import numpy as np, ml_dtypes
CORES = [1,5,17,21,33,37,49,53]
N = 8
import mx_ref
BF = ml_dtypes.bfloat16
def gentries(a):
    return np.ascontiguousarray(a.reshape(8, 16, -1).transpose(0, 2, 1)).reshape(8, -1)
def gtable(e):
    e = np.asarray(e); return np.ascontiguousarray(e.reshape(8, -1, 16).transpose(0, 2, 1)).reshape(128, -1).astype(np.int32)
def gcols(t, e):
    v = np.concatenate([t.reshape(8, 16, -1, 4), np.zeros((8, 16, 1, 4), BF)], axis=2)
    return np.ascontiguousarray(np.stack([v[g][:, e[g]] for g in range(8)])).reshape(128, -1)
def tile(rs):
    return np.stack(rs, axis=2).reshape(128, -1).astype(BF)
def pick(q, e):
    c = np.concatenate([q[0].reshape(128, -1, 4), np.zeros((128, 1, 4), np.uint8)], axis=1); s = np.concatenate([q[1], np.ones((16, 1), np.uint8)], axis=1)
    return (np.ascontiguousarray(c[:, e].reshape(128, -1)), np.ascontiguousarray(s[:, e]))
def join(*qs):
    return (np.concatenate([q[0] for q in qs], axis=1), np.concatenate([q[1] for q in qs], axis=1))
def put(q, e, v):
    c, s = q[0].reshape(128, -1, 4).copy(), q[1].copy(); c[:, e] = v[0].reshape(128, -1, 4); s[:, e] = v[1]
    return (c.reshape(128, -1), s)
def pk(c, s):
    return (np.ascontiguousarray(c), mx_ref.live(s))
def emit(q):
    return q[0], q[1]
def packed(v, rng):
    q = [mx_ref.quantize(np.ascontiguousarray(v[r])) for r in range(N)]
    return np.stack([a for a, b in q]), np.stack([mx_ref.plane(b, rng) for a, b in q])
def values_of_codes():
    e, c = np.zeros((128, 128, 4), np.float32), np.zeros((128, 2, 4), np.uint8)
    e[np.arange(128), np.arange(128), 0] = 1
    c[:127, :, 0] = np.arange(256).reshape(2, 128).T[:127]
    return mx_ref.matmul(mx_ref.quantize(e.reshape(128, 512).astype(BF)), (c.reshape(128, 8), np.full((16, 2), 127, np.uint8))).T.reshape(-1).astype(np.float64)
CODE_VALUE, SCALE_VALUE = values_of_codes(), 2.0 ** (np.arange(256) - 127.0)
def decode(q):
    return (CODE_VALUE[q[0]].reshape(16, 8, -1, 4) * SCALE_VALUE[q[1]][:, None, :, None] + 0.0).reshape(128, -1).astype(np.float32)
def f(rng, *shape):
    return mx_ref.flush((rng.standard_normal(shape, dtype=np.float32) * np.exp2(rng.integers(-2, 3, shape[:-1] + (1,)))).astype(BF))
def wide(rng, *shape, cols=0):
    v = rng.standard_normal(shape, dtype=np.float32) * np.exp2(rng.integers(-12, 13, shape)).astype(np.float32)
    if cols: v *= np.repeat(np.exp2(rng.integers(-cols, cols + 1, shape[:-2] + (1, shape[-1] // 4))) * (rng.random(shape[:-2] + (1, shape[-1] // 4)) > 0.0625), 4, axis=-1).astype(np.float32)
    return mx_ref.flush(v.astype(BF))
C, A, R = 384, 320, 3
STEP = [1, 2, 4]
def nearest(s, a, b):
    at = lambda e: np.abs(s - np.take_along_axis(s, e, axis=1))
    return np.where(at(b) < at(a), b, a)
def depths(b):
    k = np.zeros((8, C), int)
    for i in range(1, C): k[:, i] = (k[np.arange(8), b[:, i]] + 1) % 4
    return k
def gput(t, e, h):
    a, b = t.reshape(8, 16, -1, 4).copy(), h.reshape(8, 16, -1, 4)
    for g in range(8): a[g][:, e[g]] = b[g]
    return a.reshape(128, -1)
def big(v):
    v = v.astype(np.float32)
    v[np.abs(v) < np.float32(2.0 ** -16)] = 0
    return v.astype(BF)
def numbers_of(rng):
    return {"x": big(f(rng, N, 128, 4 * C)), "u": np.array(f(rng, N, 128, 512)), "v": np.array(f(rng, N, 128, 512))}
def layers(rng):
    return big(f(rng, N, 128, 2048)).reshape(N, 8, 16, 4, 8, 16, 4)
def weights(rng, w):
    c, p = packed(np.ascontiguousarray(w).reshape(N, 128, 2048), rng)
    return {"wc": c, "ws": p}
def listed(a, b):
    return np.stack([gtable(np.concatenate([a[r], b[r]], axis=1)) for r in range(N)])
def candidates(rng):
    reach = np.stack([np.where(rng.permutation(8) < 4, C, 8) for r in range(N)])[:, :, None]
    n = np.minimum(np.maximum(np.arange(C), 1), reach)
    a, b = [np.maximum(np.arange(C) - 1 - rng.integers(0, n), 0) for k in range(2)]
    return {"cd": listed(a, b)}
def signs(rng):
    return np.stack([rng.permutation(8) % 2 * 2.0 - 1.0 for r in range(N)])
def setup_inputs(rng):
    return {**numbers_of(rng), **weights(rng, layers(rng)), **candidates(rng)}
def setup_inputs_ties(rng):
    d = numbers_of(rng)
    e = rng.permutation(N)
    x = d["x"].reshape(N, 8, 16, C, 4)
    for r in range(N):
        k = np.zeros(C, int) if r == e[0] else rng.permutation(C) % 3
        a = x[r][:, :8, :3].copy()
        a[:, :, 2] = 0
        x[r][:, :8] = a[:, :, k]
    x[e[1]] = 0
    u = d["u"].reshape(N, 8, 16, 128, 4)
    u[:, :, 8:, ::16] = 0
    w = layers(rng)
    w[:, :, :, :, :, :8] = 0
    return {"x": x.reshape(N, 128, 4 * C), "u": u.reshape(N, 128, 512), "v": d["v"], **weights(rng, w), **candidates(rng)}
def setup_inputs_near(rng):
    d = numbers_of(rng)
    x = np.zeros((N, 8, 16, C, 4), np.float32)
    u = d["u"].reshape(N, 128, 128, 4)
    u[:, :, ::16] = 0
    o, c = rng.permutation(N) % 4, signs(rng)
    for r in range(N):
        m = np.full((8, 1), 256)
        m[np.argsort(c[r], kind="stable")[::2]] = 4
        s = rng.integers(0, m, (8, C))
        size = 1.0 if o[r] < 2 else 2.0 ** -7
        g = ((s[:, :, None] >> np.arange(8)) & 1) * np.exp2(np.arange(8) - 23.0) * size
        if o[r] < 3: x[r, :, 0, :, 0] = c[r][:, None] * rng.integers(0, 2, (8, C)) * size
        x[r, :, 8] = g[:, :, :4]
        x[r, :, 9] = g[:, :, 4:]
        x[r, :, 10:] = rng.integers(4, 8, (8, 6, C, 4)) * 2.0 ** -22 * size
        k = 1.0 if o[r] == 0 else 2.0 ** -30
        for h in range(0, 128, 16):
            u[r, h, h, 0] = k
            u[r, h + 8:h + 10, h] = k
    w = layers(rng)
    w[:, :, :10] = 0
    w[:, :, :, :, :, :10] = 0
    return {"x": x.reshape(N, 128, 4 * C).astype(BF), "u": u.reshape(N, 128, 512), "v": d["v"], **weights(rng, w), **candidates(rng)}
def setup_inputs_huge(rng):
    d = numbers_of(rng)
    z = rng.permutation(N) < N // 2
    k = np.stack([rng.choice([-1.0, -0.25] if z[r] else [-1.0, -0.5, 0.5, 1.0], C) for r in range(N)])
    x = 2.0 ** 28 * (0.8 + 0.2 * rng.random((N, 128, C, 4))) * k[:, None, :, None]
    u = d["u"].reshape(N, 128, 128, 4)
    a = 2.0 ** 30 * (1 - 0.25 * rng.random((N, 128, 8, 4))) * signs(rng)[:, None, :, None]
    u[:, :, ::16] = a.astype(np.float32).astype(BF)
    w = np.zeros((N, 128, 4, 128, 4), np.float32)
    i = np.arange(128)
    for b in range(4): w[:, i, b, i, b] = -1
    return {"x": x.astype(np.float32).reshape(N, 128, 4 * C).astype(BF), "u": u.reshape(N, 128, 512), "v": d["v"], **weights(rng, w.astype(BF)), **candidates(rng)}
def shape(rng, k):
    if k == 0: return np.maximum(np.arange(C) - 1, 0)
    if k == 1: return np.zeros(C, int)
    if k == 8:
        b = np.full(C, 1)
        b[:2] = 0
        return b
    if k == 9:
        n = A - 24
        b = np.full(C, 3)
        b[:4] = 0, 0, 1, 2
        b[n + 3:n + 11] = n - 5 + rng.permutation(8)
        b[n + 11:n + 19] = n + 3 + rng.permutation(8)
        b[n + 19:] = n + 11 + rng.integers(0, 8, C - n - 19)
        return b
    n = [C - 3, A, A - 1, A + 1, A - 2, 1][k - 2]
    b = rng.integers(0, 3, C) if k in (3, 4, 5) else np.full(C, 2)
    b[:4] = 0, 0, 1, 2
    b[4 + rng.permutation(C - 4)[:n - 1]] = 3
    return b
def setup_inputs_trees(rng):
    d = setup_inputs(rng)
    m = rng.permutation(10)
    b = np.stack([np.stack([shape(rng, k) for k in rng.permutation(np.delete(np.arange(10), [m[r], m[r - 1]]))]) for r in range(N)])
    d["cd"] = listed(b, b)
    return d
def setup_inputs_spread(rng):
    d = setup_inputs(rng)
    d["x"] = big(wide(rng, N, 128, 4 * C, cols=6))
    return d
def check_inputs(d):
    b = []
    for k in ("x", "u", "v"):
        a = np.abs(d[k].astype(np.float32))
        if not (np.isfinite(a).all() and ((a == 0) | (a >= 2.0 ** -30) & (a <= 2.0 ** 30)).all()): b.append("a value of " + k)
    none, least, most = [emit(mx_ref.quantize(np.full((128, 16), k, np.float32).astype(BF)))[1][0, 0] for k in (0.0, 2.0 ** -30, 2.0 ** 30)]
    for r in range(N):
        if ((d["wc"][r] == 0x7F) | (d["wc"][r] == 0xFF)).any(): b.append("wc: a code that is no number")
        s = mx_ref.live(d["ws"][r])
        if ((s != none) & ((s < least) | (s > most))).any(): b.append("ws: a scale out of range")
        e = gentries(d["cd"][r]).reshape(8, 2, C)
        if ((e < 0) | (e > np.maximum(np.arange(C) - 1, 0))).any(): b.append("cd: a candidate that isn't lower")
    return b
def reference(x, u, v, wc, ws, cd):
    qu = [mx_ref.quantize(u[r]) for r in range(N)]
    lay = [pk(wc[r], ws[r]) for r in range(N)]
    can = [gentries(cd[r]) for r in range(N)]
    now = [x[r] for r in range(N)]
    for t in range(R):
        held, took, depth, base, sent = [], [], [], [], []
        for r in range(N):
            q = mx_ref.quantize(now[r])
            b = nearest(mx_ref.matmul(qu[r], q)[::16], can[r][:, :C], can[r][:, C:])
            k = depths(b)
            o = np.argsort(k, axis=1, kind="stable")[:, :A]
            place = np.zeros((8, C), int)
            np.put_along_axis(place, o, np.arange(A)[None], axis=1)
            k, b = np.take_along_axis(k, o, axis=1), np.take_along_axis(b, o, axis=1)
            h = decode(q).astype(BF)
            p = gcols(h, o).astype(np.float32) - gcols(h, np.where(k > 0, b, -1)).astype(np.float32)
            sent.append(mx_ref.quantize(p.astype(BF)))
            held.append(h)
            took.append(o)
            depth.append(k)
            base.append(np.take_along_axis(place, b, axis=1))
        made = []
        for r in range(N):
            e = (r - STEP[t]) % N
            m = decode(sent[e]).astype(BF)
            for k in (1, 2, 3): m = (m.astype(np.float32) + gcols(m, np.where(depth[e] == k, base[e], -1)).astype(np.float32)).astype(BF)
            q = mx_ref.quantize(m)
            z = gcols(held[r], took[r])
            h = tile([mx_ref.matmul(pick(lay[r], np.arange(128 * b, 128 * b + 128)), q) * np.float32(0.015625) + z[:, b::4].astype(np.float32) for b in range(4)])
            made.append(gput(held[r], took[r], h))
        now = made
    y = np.zeros((N, 128, C), np.float32)
    oc, osc = np.zeros((N, 128, 4 * C), np.uint8), np.zeros((N, 16, C), np.uint8)
    for r in range(N):
        q = mx_ref.quantize(now[r])
        y[r] = mx_ref.matmul(mx_ref.quantize(v[r]), q)
        oc[r], osc[r] = emit(q)
    return {"y": y, "oc": oc, "osc": osc}

@@ -1,0 +1,399 @@
+from concourse.mybir import dt, AluOpType, ActivationFunctionType
+
+C, A, R, N = 384, 320, 3, 8
+STEP = [1, 2, 4]
+Q, M = 24, 16
+PW = 400
+RW = 336
+YW = 528
+F4, U8 = "float8_e4m3fn_x4", "uint8"
+
+WIDTHS = {
+    "bfloat16": {"xt0": 4 * C, "ut": 512, "vt": 512, "one": 512, "onen": 512, "et": 2048, "en": 2048, "dg": 768, "rs": 1152, "rq": 96,
+                 "mk": 256, "jid": C, "tb": 128, "tv": 128, "of": C, "og": A, "oh": A, "fp": 4 * PW, "fn": 4 * PW, "fm2": 4 * PW,
+                 "pt": 4 * C, "ma": 4 * PW, "mb": 4 * PW, "mc": 4 * PW, "md": 4 * PW, "mt": 4 * A, "xt": 4 * C},
+    "float32": {"zero": 16, "w1": 256, "w2": 256, "tbl": 400, "i6": C, "sb": PW, "c1": 1152, "c2": 1152, "da": 48, "db": 48, "dc": 48,
+                "se": 24, "sm": 72, "sx": 72, "bz": 24, "own": C, "y1": YW, "d2": YW, "ind": 96, "inc": 96, "ls": 96, "pos": 24,
+                "bs": 256, "pu": 96, "pl": 24, "rp": 4 * RW, "yo": C},
+    "int32": {"cdf": 768, "dw": 24, "dm": 24},
+    "uint16": {"lin": 48, "lex": 24, "lb": 30, "lpl": 24, "lpx": 24},
+    F4: {"wq": 512, "uq": 128, "urq": 128, "vq": 128, "xq": C, "eq": 512, "nq": 512, "pq": C, "mq": A, "oq": C},
+    U8: {"wp": 512, "up": 128, "urp": 128, "vp": 128, "xp": C, "ep": 512, "npl": 512, "pz": C, "mp": A, "op": C},
+}
+SCRATCH = {n: ("sbuf", [128, w], k) for k, m in WIDTHS.items() for n, w in m.items()}
+SCRATCH["psA"] = SCRATCH["psB"] = ("psum", [128, 2048], "float32")
+GROUPS = {
+    "ic_": ("int32", {"pi": 1, "pm": 1, "pp": 1, "ia": 16, "ib": 16, "ic": 24, "i1": 30, "i2": 16, "i3": 24, "i8": 8, "i9": 8,
+                      "n1": 24, "n2": 24, "n3": 24, "i4": 64, "i5": 64, "k1": 48, "k2": 48, "k3": 48, "ke": 48}),
+    "fc_": ("float32", {"fm": 1, "f24": 1, "f32m": 1, "f16m": 1, "f16p": 1, "fr": 1, "w3": 64, "w4": 64, "w5": 64,
+                        "kf": 48, "kg": 48, "ks": 48, "sel1": 72, "sel2": 72, "seld": 72}),
+    "lk_": ("uint16", {"lnat": 24, "lback": 24, "lu": 8, "lcd": 48, "ly": 30, "ld": 24, "ltot": 8, "ldup": 16, "lc": 48}),
+}
+PART = {}
+for _g, (_k, _m) in GROUPS.items():
+    _a = 0
+    for _s, _n in _m.items():
+        PART[_s] = (_g, _a, _n)
+        _a += _n + _n % 2
+    SCRATCH[_g] = ("sbuf", [128, _a], _k)
+for _t in range(R + 1):
+    SCRATCH["tq%d" % _t] = ("sbuf", [128, C], F4)
+    SCRATCH["tp%d" % _t] = ("sbuf", [128, C], U8)
+SENT = [("tq", "aq", F4, C), ("tp", "ap", U8, C), ("ql", "al", "uint16", 24), ("qo", "ao", "uint16", 20)]
+for _t in range(R):
+    for _s, _d, _k, _n in SENT:
+        if _s[0] == "q": SCRATCH["%s%d" % (_s, _t)] = ("sbuf", [128, _n], _k)
+        SCRATCH["%s%d" % (_d, _t)] = ("sbuf", [128, _n], _k)
+NDMA = 12
+SEMAPHORES = ["cv", "cs", "ct", "cg"] + ["d%d" % k for k in range(NDMA)] + ["%s_%s%d" % (a, b[0][1], t) for a in ("r", "l") for b in SENT for t in range(R)]
+
+
+def rank_program(g, core, T, topo):
+    rank = T.rank_of(core)
+    if rank is None:
+        return
+    OP, AF = AluOpType, ActivationFunctionType
+    eng = {"v": g.vector, "s": g.scalar, "t": g.tensor, "g": g, "y": g.sync}
+    csem = {"v": "cv", "s": "cs", "t": "ct", "g": "cg"}
+    count = {}
+    known = {q: {} for q in eng}
+    known["far"] = {}
+    log = {}
+    serial = [0]
+
+    def apart(r, o):
+        if r[2] <= o[1] or o[2] <= r[1]: return True
+        return r[3] > 1 and r[3] == o[3] and (r[1] - o[1]) % r[3] != 0
+
+    def widen(r):
+        return (r[0], r[1] // 512 * 512, (r[2] + 511) // 512 * 512, 1) if r[0][:2] == "ps" else r
+
+    def settle(q, reads, writes):
+        need = {}
+        for w, rs in ((False, reads), (True, writes)):
+            for r in rs:
+                bank = r[0][:2] == "ps"
+                for o in log.get(r[0], ()):
+                    if apart(widen(r), o["r"]): continue
+                    if not (w or o["w"]) and not (bank and o["q"] != q): continue
+                    need[o["n"]] = o
+        for n in sorted(need, reverse=True):
+            o = need[n]
+            if known[q].get(o["sem"], 0) >= o["val"]: continue
+            eng[q].wait_ge(T.sem[o["sem"]], o["val"])
+            for k, v in list(o["clock"].items()) + [(o["sem"], o["val"])]:
+                known[q][k] = max(known[q].get(k, 0), v)
+
+    def note(q, reads, writes, sem, val):
+        serial[0] += 1
+        clock = dict(known[q])
+        for w, rs in ((False, reads), (True, writes)):
+            for r in rs:
+                r = widen(r)
+                old = log.get(r[0], [])
+                if w and r[3] == 1: old = [o for o in old if not (r[1] <= o["r"][1] and o["r"][2] <= r[2])]
+                log[r[0]] = old + [{"r": r, "w": w, "q": q, "sem": sem, "val": val, "clock": clock, "n": serial[0]}]
+
+    def run(q, call, reads, writes):
+        settle(q, reads, writes)
+        s = csem[q]
+        count[s] = count.get(s, 0) + 1
+        call().then_inc(T.sem[s], 1)
+        note(q, reads, writes, s, count[s])
+
+    def B(name, a=0, b=None, step=1):
+        if name in PART:
+            p, o, n = PART[name]
+            return (p, o + a, o + (n if b is None else b), step)
+        return (name, a, SCRATCH[name][1][1] if b is None else b, step)
+
+    def ap(r):
+        return T[r[0]][:, r[1]:r[2]] if r[3] == 1 else T[r[0]][:, r[1]:r[2]:r[3]]
+
+    def ind(r, off): return ap(r).indirect(ap(off))
+    def sc(x): return ap(x) if isinstance(x, tuple) else x
+    def rd(*xs): return [x for x in xs if isinstance(x, tuple)]
+
+    def fill(out, c): run("v", lambda: g.vector.memset(ap(out), c), [], [out])
+    def copy(out, i): run("v", lambda: g.vector.tensor_copy(ap(out), ap(i)), [i], [out])
+    def copyi(out, i, off): run("v", lambda: g.vector.tensor_copy(ap(out), ind(i, off)), [i, off], [out])
+    def tt(out, a, b, op): run("v", lambda: g.vector.tensor_tensor(ap(out), ap(a), ap(b), op), [a, b], [out])
+    def tti(out, a, off, b, op): run("v", lambda: g.vector.tensor_tensor(ap(out), ind(a, off), ap(b), op), [a, off, b], [out])
+    def ts(out, a, s1, op, s2=None, op1=None):
+        if op1 is None: run("v", lambda: g.vector.tensor_scalar(ap(out), ap(a), sc(s1), None, op), [a] + rd(s1), [out])
+        else: run("v", lambda: g.vector.tensor_scalar(ap(out), ap(a), sc(s1), sc(s2), op, op1), [a] + rd(s1, s2), [out])
+    def scan(out, keep, a): run("v", lambda: g.vector.tensor_tensor_scan(ap(out), ap(keep), ap(a), 0.0, OP.mult, OP.add), [keep, a], [out])
+    def quant(q, p, i): run("v", lambda: g.vector.quantize_mx(ap(q), ap(p), ap(i)), [i], [q, p])
+    def mm(out, a, asc, b, bsc): run("t", lambda: g.tensor.matmul_mx(ap(out), ap(a), ap(asc), ap(b), ap(bsc), True, True), [a, asc, b, bsc], [out])
+    def act(out, i): run("s", lambda: g.scalar.activation(ap(out), ap(i), AF.Copy), [i], [out])
+    def actm(out, i, k): run("s", lambda: g.scalar.activation(ap(out), ap(i), AF.Copy, scale=k), [i], [out])
+    def acti(out, i, off): run("s", lambda: g.scalar.activation(ap(out), ind(i, off), AF.Copy), [i, off], [out])
+    def pick(q, p, i, ip, off):
+        run("v", lambda: g.vector.tensor_copy(ap(q).bitcast(dt.uint32), ap(i).bitcast(dt.uint32).indirect(ap(off))), [i, off], [q])
+        acti(p, ip, off)
+    def iota(out, pattern, base, cm): run("g", lambda: g.iota(ap(out), pattern, base, cm), [], [out])
+    def iotaf(out, pattern, base, cm): run("g", lambda: g.iota(ap(out), pattern, base, cm, allow_small_or_imprecise_dtypes=True), [], [out])
+    def units(name, ones):
+        for b in range(4):
+            o = B(name, 512 * b, 512 * b + 512)
+            run("g", lambda: g.affine_select(ap(o), ap(B(ones)), [[1, 512]], OP.is_equal, 0.0, -b, -4), [B(ones)], [o])
+    ndma = [0]
+
+    def dma(pairs, reads, writes):
+        s = "d%d" % ndma[0]
+        ndma[0] += 1
+        for q in sorted({p[0] for p in pairs}): settle(q, reads, writes)
+        for q, o, i in pairs: eng[q].dma_start(o, i).then_inc(T.sem[s], 16)
+        count[s] = 16 * len(pairs)
+        note(pairs[0][0], reads, writes, s, count[s])
+
+    def send(k, t):
+        s, d, kind, n = SENT[k]
+        dst, src = T.cores[(rank + STEP[t]) % N], "%s%d" % (s, t)
+        settle("g", [B(src)], [])
+        i, o = T[src][:, :], T["%s%d" % (d, t)][:, :]
+        if kind == F4: i, o = i.bitcast(dt.uint8), o.bitcast(dt.uint8)
+        ls, to = "l_%s%d" % (s[1], t), topo.addr(dst)
+        g.remote_dma(o, i, T.sem["r_%s%d" % (s[1], t)], T.sem[ls], to[1], to[0], topo.mask(core, dst))
+        count[ls] = len(topo.engines(core, dst))
+
+    def expect(k, t):
+        s, d, kind, n = SENT[k]
+        rs = "r_%s%d" % (s[1], t)
+        count[rs] = len(topo.engines(T.cores[(rank - STEP[t]) % N], core))
+        note("far", [], [B("%s%d" % (d, t))], rs, count[rs])
+
+    def plane(name, b): return B(name, PW * b, PW * b + PW)
+    def body(name, b): return B(name, PW * b, PW * b + C)
+    def side(name, b): return B(name, 128 * b, 128 * b + 128)
+
+    dma([("y", T.xt0[:, :], T.x[:, :])], [], [B("xt0")])
+    dma([("s", T.ut[:, :], T.u[:, :])], [], [B("ut")])
+    dma([("ys"[k % 2], T.cdf[k:128:16, :], T.cd[:, :]) for k in range(16)], [], [B("cdf")])
+    settle("y", [B("xt0")], [])
+    settle("s", [B("ut"), B("cdf")], [])
+    dma([("y", T.wq[:, :].bitcast(dt.uint8), T.wc[:, :])], [], [B("wq")])
+    dma([("s", T.wp[:, :], T.ws[:, :])], [], [B("wp")])
+    dma([("s", T.vt[:, :], T.v[:, :])], [], [B("vt")])
+
+    iota(B("pi"), [[0, 1]], 0, 1)
+    iota(B("ic"), [[1, 24]], 0, 0)
+    iota(B("i8"), [[16, 8]], 0, 0)
+    iota(B("ia"), [[1, 16]], 128, -1)
+    iota(B("ib"), [[1, 16]], 0, 0)
+    iota(B("i1"), [[1, 15], [256, 2]], 17, 0)
+    iota(B("i9"), [[24, 4], [0, 2]], 23, 0)
+    iota(B("i2"), [[32, 4], [0, 2], [16, 2]], 0, 0)
+    iota(B("i4"), [[0, 2], [1, 32]], 0, 0)
+    iota(B("i5"), [[1, 2], [0, 32]], 0, 0)
+    iota(B("i3"), [[16, 24]], 0, 0)
+    iotaf(B("i6"), [[1, 24], [32, 16]], 16, 0)
+    fill(B("one"), 1.0)
+    units("et", "one")
+    ts(B("pm"), B("pi"), 15, OP.bitwise_and)
+    copy(B("fm"), B("pm"))
+    ts(B("f24"), B("pm"), 24.0, OP.mult)
+    ts(B("lnat"), B("ic"), B("f24"), OP.add)
+    copy(B("lu"), B("i8"))
+    ts(B("ia"), B("ia"), 15, OP.bitwise_and)
+    ts(B("dg", 0, 16), B("ia"), 0.0, OP.is_equal)
+    ts(B("rs", 0, 16), B("ib"), 0.0, OP.is_gt)
+    ts(B("rq", 0, 24), B("ic"), 0.0, OP.is_gt)
+    for name, n, w in (("dg", 768, 16), ("rs", 1152, 16), ("rq", 96, 24)):
+        while w < n:
+            k = min(w, n - w)
+            copy(B(name, w, w + k), B(name, 0, k))
+            w += k
+    ts(B("n1"), B("ic"), B("f24"), OP.add)
+    ts(B("n2"), B("n1"), 15, OP.bitwise_and)
+    ts(B("n3"), B("n1"), 4, OP.arith_shift_right)
+    ts(B("n2"), B("n2"), 48.0, OP.mult)
+    tt(B("n2"), B("n2"), B("n3"), OP.add)
+    copy(B("lcd", 0, 24), B("n2"))
+    ts(B("lcd", 24, 48), B("n2"), 24.0, OP.add)
+    quant(B("uq"), B("up"), B("ut"))
+    pick(B("urq"), B("urp"), B("uq"), B("up"), B("lu"))
+    fill(B("zero"), 0.0)
+    fill(B("onen"), -1.0)
+    fill(B("sb", C, PW), 0.0)
+
+    def lists_of_candidates():
+        tti(B("c1", 0, 768), B("cdf"), B("lcd"), B("dg"), OP.mult)
+        scan(B("c2", 0, 768), B("rs", 0, 768), B("c1", 0, 768))
+        copy(B("k1"), B("c2", 15, 768, 16))
+        ts(B("k2"), B("k1"), 2731.0, OP.mult)
+        ts(B("k2"), B("k2"), 16, OP.arith_shift_right)
+        ts(B("k2"), B("k2"), -383.0, OP.mult)
+        ts(B("k3"), B("k1"), 16.0, OP.mult)
+        tt(B("ke"), B("k2"), B("k3"), OP.add)
+        ts(B("fr"), B("fm"), 0.0, OP.is_equal, 385.0, OP.mult)
+        for h in (0, 24): tt(B("ke", h, h + 1), B("ke", h, h + 1), B("fr"), OP.add)
+        copy(B("lc"), B("ke"))
+
+    def lists_inside():
+        ts(B("k2"), B("ke"), 15, OP.bitwise_and)
+        ts(B("kf"), B("k2"), B("fm"), OP.is_equal)
+        ts(B("kg"), B("kf"), -1.0, OP.mult, 1.0, OP.add)
+        ts(B("ks"), B("ke"), -386.0, OP.add)
+        ts(B("k3"), B("ke"), 16.0, OP.add)
+        for h, s in ((0, "sel1"), (24, "sel2")):
+            copy(B(s, 0, 24), B("ke", h, h + 24))
+            tt(B(s, 24, 48), B("k3", h, h + 24), B("kf", h, h + 24), OP.mult)
+            tt(B(s, 48, 72), B("ks", h, h + 24), B("kg", h, h + 24), OP.mult)
+            ts(B(s, 48, 72), B(s, 48, 72), 386.0, OP.add)
+        tt(B("seld"), B("sel2"), B("sel1"), OP.subtract)
+
+    def table():
+        iotaf(B("jid"), [[1, C]], -192, 0)
+        units("en", "onen")
+        fill(B("tbl", C, PW), 0.0)
+        fill(B("tbl", 386, 387), 0.0009765625)
+        run("s", lambda: g.scalar.activation(ap(B("tbl", 0, C)), ap(B("i6")), AF.Identity, bias=0.0009765625), [B("i6")], [B("tbl", 0, C)])
+
+    def late_constants():
+        fill(B("y1", 0, 16), 0.0)
+        fill(B("y1", 400, YW), 0.0)
+        fill(B("d2", 0, 16), 0.0)
+        ts(B("f16m"), B("pm"), 16.0, OP.mult)
+        ts(B("f32m"), B("pm"), 32.0, OP.mult)
+        ts(B("ly"), B("i1"), B("f16m"), OP.add)
+        ts(B("ld"), B("ic"), B("f32m"), OP.add, 16.0, OP.add)
+        copy(B("ltot"), B("i9"))
+        ts(B("ldup"), B("i2"), B("fm"), OP.add)
+        ts(B("pp"), B("pi"), 4, OP.arith_shift_right, 1, OP.bitwise_and)
+        ts(B("f16p"), B("pp"), 16.0, OP.mult)
+        ts(B("w4"), B("i4"), B("f16p"), OP.subtract)
+        ts(B("w5"), B("w4"), B("fm"), OP.is_lt)
+        tt(B("w5"), B("w5"), B("i5"), OP.not_equal)
+        ts(B("w3"), B("w4"), 0.0, OP.is_ge)
+        tt(B("w5"), B("w5"), B("w3"), OP.mult)
+        ts(B("w3"), B("w4"), 15.0, OP.is_le)
+        tt(B("mk", 0, 64), B("w5"), B("w3"), OP.mult)
+        copy(B("mk", 64, 128), B("mk", 0, 64))
+        copy(B("mk", 128, 256), B("mk", 0, 128))
+        fill(B("w2"), 1.0)
+        for b in range(4):
+            for name in ("fn", "ma", "mb", "mc"): act(B(name, PW * b + C, PW * b + PW), B("zero"))
+            act(B("rp", RW * b + A, RW * b + RW), B("zero"))
+
+    def last_constants():
+        ts(B("n1"), B("i3"), B("fm"), OP.add)
+        ts(B("n2"), B("n1"), 2731.0, OP.mult)
+        ts(B("n2"), B("n2"), 16, OP.arith_shift_right)
+        ts(B("n2"), B("n2"), -383.0, OP.mult)
+        ts(B("n3"), B("n1"), 16.0, OP.mult)
+        tt(B("n3"), B("n2"), B("n3"), OP.add)
+        copy(B("lback"), B("n3"))
+        quant(B("vq"), B("vp"), B("vt"))
+
+    for t in range(R):
+        tq, tp, aq, apl, al, ao = ["%s%d" % (s, t) for s in ("tq", "tp", "aq", "ap", "al", "ao")]
+        if t == 0:
+            quant(B("xq"), B("xp"), B("xt0"))
+            pick(B(tq), B(tp), B("xq"), B("xp"), B("lnat"))
+        else:
+            for h in (0, 192): quant(B(tq, h, h + 192), B(tp, h, h + 192), B("xt", 4 * h, 4 * h + 768))
+        for h, k in ((0, 0), (192, 512)):
+            mm(B("psA", k, k + 192), B("urq"), B("urp"), B(tq, h, h + 192), B(tp, h, h + 192))
+            act(B("sb", h, h + 192), B("psA", k, k + 192))
+        send(0, t)
+        send(1, t)
+        if t == 0:
+            lists_of_candidates()
+            table()
+        tti(B("c1", 0, 768), B("sb"), B("lc"), B("dg"), OP.mult)
+        for h, k in ((0, 0), (192, 512)): tt(B("c1", 768 + h, 960 + h), B("psA", k, k + 192), B("dg", 0, 192), OP.mult)
+        scan(B("c2"), B("rs"), B("c1"))
+        if t == 0:
+            lists_inside()
+            quant(B("eq"), B("ep"), B("et"))
+        for h in (0, 24): tt(B("da", h, h + 24), B("c2", 16 * h + 15, 16 * h + 384, 16), B("c2", 783, 1152, 16), OP.subtract)
+        ts(B("db"), B("da"), -1.0, OP.mult)
+        tt(B("dc"), B("da"), B("db"), OP.max)
+        tt(B("se"), B("dc", 24, 48), B("dc", 0, 24), OP.is_lt)
+        for h in (48, 24, 0): tt(B("sm", h, h + 24), B("seld", h, h + 24), B("se"), OP.mult)
+        tt(B("sx"), B("sm"), B("sel1"), OP.add)
+        copy(B("lex"), B("sx", 48, 72))
+        copy(B("lin", 0, 48, 2), B("sx", 24, 48))
+        ts(B("bz"), B("sx", 0, 24), -float(C), OP.add)
+        acti(B("own", 0, 64), B("tbl"), B("lex", 0, 4))
+        acti(B("own", 64, C), B("tbl"), B("lex", 4, 24))
+        for b in range(4):
+            mm(B("psB", 512 * b, 512 * b + C), side("eq", b), side("ep", b), B(tq), B(tp))
+            act(body("fp", b), B("psB", 512 * b, 512 * b + C))
+        if t == 0: late_constants()
+        copy(B("y1", 16, 32), B("own", 0, 16))
+        for q in range(1, Q):
+            tti(B("y1", 16 + 16 * q, 32 + 16 * q), B("y1", 0, 16 + 16 * q), B("lin", 2 * q, 2 * q + 1), B("own", 16 * q, 16 * q + 16), OP.add)
+        if t == 0: quant(B("nq"), B("npl"), B("en"))
+        tti(B("c1", 0, 480), B("y1"), B("ly"), B("dg", 0, 480), OP.mult)
+        scan(B("c2", 0, 480), B("rs", 0, 480), B("c1", 0, 480))
+        copy(B("lb"), B("c2", 15, 480, 16))
+        copy(B("d2", 16, 48), B("y1", 16, YW, 16))
+        for m in range(1, M):
+            tti(B("d2", 16 + 32 * m, 48 + 32 * m), B("d2", 0, 16 + 32 * m), B("lb", 2 * m - 2, 2 * m), B("y1", 16 + m, YW, 16), OP.add)
+        tti(B("c1", 0, C), B("d2"), B("ld"), B("dg", 0, C), OP.mult)
+        scan(B("c2", 0, C), B("rs", 0, C), B("c1", 0, C))
+        ts(B("dw"), B("c2", 15, C, 16), 1024.0, OP.mult)
+        ts(B("dm"), B("dw"), 3, OP.bitwise_and)
+        ts(B("pos"), B("dm"), 0.0, OP.is_gt)
+        tt(B("ls", 0, 24), B("bz"), B("pos"), OP.mult)
+        ts(B("ql%d" % t), B("ls", 0, 24), float(C), OP.add)
+        send(2, t)
+        for c in range(4): ts(B("ind", 24 * c, 24 * c + 24), B("dm"), float(c), OP.is_equal)
+        scan(B("inc"), B("rq"), B("ind"))
+        copyi(B("tb"), B("inc"), B("ltot"))
+        run("v", lambda: g.vector.transpose(ap(B("tv")), ap(B("tb"))), [B("tb")], [B("tv")])
+        tti(B("w1"), B("tv"), B("ldup"), B("mk"), OP.mult)
+        scan(B("bs"), B("w2"), B("w1"))
+        for c in range(4): ts(B("pu", 24 * c, 24 * c + 24), B("inc", 24 * c, 24 * c + 24), B("bs", 64 * c + 31, 64 * c + 32), OP.add, -1.0, OP.add)
+        tt(B("ls"), B("pu"), B("ind"), OP.mult)
+        tt(B("pu", 0, 48), B("ls", 0, 48), B("ls", 48, 96), OP.add)
+        tt(B("pl"), B("pu", 0, 24), B("pu", 24, 48), OP.add)
+        copy(B("lpl"), B("pl"))
+        run("v", lambda: g.vector.tensor_copy(ind(B("of"), B("lpl")), ap(B("jid"))), [B("jid"), B("lpl")], [B("of")])
+        ts(B("lpx"), B("pl"), float(A), OP.min)
+        for k in range(4): expect(k, t)
+        for b in range(4):
+            mm(B("psA", 512 * b, 512 * b + C), side("nq", b), side("npl", b), B(aq), B(apl))
+            act(body("fn", b), B("psA", 512 * b, 512 * b + C))
+            act(body("fm2", b), B("psA", 512 * b, 512 * b + C))
+        for b in range(4):
+            tti(B("pt", b, 4 * C, 4), plane("fn", b), B(al), body("fm2", b), OP.subtract)
+        for h, ps in ((0, "psB"), (192, "psA")):
+            quant(B("pq", h, h + 192), B("pz", h, h + 192), B("pt", 4 * h, 4 * h + 768))
+            mm(B(ps, 0, 192), side("eq", 0), side("ep", 0), B("pq", h, h + 192), B("pz", h, h + 192))
+            act(B("ma", h, h + 192), B(ps, 0, 192))
+        for h, ps in ((0, "psB"), (192, "psA")): act(B("md", h, h + 192), B(ps, 0, 192))
+        for b in range(1, 4):
+            mm(B("psB", 512 * b, 512 * b + C), side("eq", b), side("ep", b), B("pq"), B("pz"))
+            for name in ("ma", "md"): act(body(name, b), B("psB", 512 * b, 512 * b + C))
+        tt(B("og"), B("of", 0, A), B("dg", 0, A), OP.mult)
+        scan(B("oh"), B("rs", 0, A), B("og"))
+        ts(B("qo%d" % t), B("oh", 15, A, 16), 192.0, OP.add)
+        send(3, t)
+        for b in range(4):
+            for src, dst in (("ma", "mb"), ("mb", "mc"), ("mc", "mb")):
+                tti(body(dst, b), plane(src, b), B(al), body("md", b), OP.add)
+            if b < 3: acti(B("mt", b, 4 * A, 4), plane("mb", b), B(ao))
+        acti(B("mt", 3, 640, 4), plane("mb", 3), B(ao, 0, 10))
+        copyi(B("mt", 643, 1280, 4), plane("mb", 3), B(ao, 10, 20))
+        for h, ps in ((0, "psA"), (160, "psB")):
+            quant(B("mq", h, h + 160), B("mp", h, h + 160), B("mt", 4 * h, 4 * h + 640))
+            mm(B(ps, 0, 160), side("wq", 0), side("wp", 0), B("mq", h, h + 160), B("mp", h, h + 160))
+            actm(B("rp", h, h + 160), B(ps, 0, 160), 0.015625)
+        if t == R - 1: last_constants()
+        for b in range(1, 4):
+            mm(B("psA", 512 * b, 512 * b + A), side("wq", b), side("wp", b), B("mq"), B("mp"))
+            actm(B("rp", RW * b, RW * b + A), B("psA", 512 * b, 512 * b + A), 0.015625)
+        for b in range(4):
+            tti(B("xt", b, 4 * C, 4), B("rp", RW * b, RW * b + RW), B("lpx"), body("fp", b), OP.add)
+
+    quant(B("tq%d" % R), B("tp%d" % R), B("xt"))
+    pick(B("oq"), B("op"), B("tq%d" % R), B("tp%d" % R), B("lback"))
+    dma([("y", T.oc[:, :], T.oq[:, :].bitcast(dt.uint8))], [B("oq")], [])
+    dma([("s", T.osc[4 * k:4 * k + 4, :], T.op[32 * k:32 * k + 4, :]) for k in range(4)], [B("op")], [])
+    mm(B("psB", 0, C), B("vq"), B("vp"), B("oq"), B("op"))
+    copy(B("yo"), B("psB", 0, C))
+    dma([("y", T.y[:, :], T.yo[:, :])], [B("yo")], [])
+    for s in sorted(count): g.wait_ge(T.sem[s], count[s])

@@ -6,36 +6,43 @@ Q, M = 24, 16
 PW = 400
 RW = 336
 YW = 528
+UNIT = 0.0009765625
 F4, U8 = "float8_e4m3fn_x4", "uint8"
 
+LISTS = [("lnat", 24, [[1, 24]], 0, 24),
+         ("lu", 8, [[16, 8]], 0, 0), ("ltot", 8, [[32, 4], [0, 2]], 31, 0),
+         ("ly", 30, [[1, 15], [256, 2]], 17, 16),
+         ("ld", 24, [[1, 24]], 16, 32),
+         ("ldup", 16, [[32, 4], [0, 2], [16, 2]], 0, 1), ("lcls", 8, [[0, 4], [16, 2]], 0, 1),
+         ("an", 48, [[256, 24], [0, 2]], 0, 6144), ("al", 24, [[2736, 24]], 0, 171),
+         ("bn", 48, [[48, 24], [24, 2]], 0, 1152), ("bl", 24, [[256, 24]], 0, 16),
+         ("ep", 48, [[32, 12], [1000, 2], [0, 2]], -1000, 1)]
+LAT, _a = {}, 0
+for _s, _n, _p, _b, _k in LISTS:
+    LAT[_s] = (_a, _a + _n)
+    _a += _n
+LW, LU = _a, LAT["an"][0]
+
 WIDTHS = {
-    "bfloat16": {"xt0": 4 * C, "ut": 512, "vt": 512, "one": 512, "onen": 512, "et": 2048, "en": 2048, "dg": 768, "rs": 1152, "rq": 96,
-                 "mk": 256, "jid": C, "tb": 128, "tv": 128, "of": C, "og": A, "oh": A, "fp": 4 * PW, "fn": 4 * PW, "fm2": 4 * PW,
+    "bfloat16": {"xt0": 4 * C, "ut": 512, "vt": 512, "one": 512, "onen": 512, "et": 2048, "en": 2048, "dg": 768, "rs": 1152, "rq": 128, "r5": 120,
+                 "mk": 256, "jid": C, "tb": 128, "tv": 128, "of": C, "og": A, "oh": A, "fp": 4 * PW, "fn": 4 * PW, "fo": 4 * PW,
                  "pt": 4 * C, "ma": 4 * PW, "mb": 4 * PW, "mc": 4 * PW, "md": 4 * PW, "mt": 4 * A, "xt": 4 * C},
-    "float32": {"zero": 16, "w1": 256, "w2": 256, "tbl": 400, "i6": C, "sb": PW, "c1": 1152, "c2": 1152, "da": 48, "db": 48, "dc": 48,
-                "se": 24, "sm": 72, "sx": 72, "bz": 24, "own": C, "y1": YW, "d2": YW, "ind": 96, "inc": 96, "ls": 96, "pos": 24,
-                "bs": 256, "pu": 96, "pl": 24, "rp": 4 * RW, "yo": C},
-    "int32": {"cdf": 768, "dw": 24, "dm": 24},
-    "uint16": {"lin": 48, "lex": 24, "lb": 30, "lpl": 24, "lpx": 24},
+    "float32": {"zero": 16, "w1": 256, "w2": 256, "tbl": 800, "i6": C, "cls": 128, "sb": PW, "c1": 1152, "c2": 1152,
+                "own": 16 + C, "y1": YW, "d2": YW, "ind": 128, "inc": 128, "bs": 256, "pu": 120, "pv": 120, "rp": 4 * RW, "yo": C},
+    "int32": {"cdf": 768, "dw": 24, "dm": 32, "pi": 1, "pm": 3, "ia": 768, "jj": 32, "li": LW, "lj": LW, "lk": LW, "lv": 72, "lw": 72, "lx": 72, "co": 72,
+              "k1": 48, "k2": 48, "k3": 48, "ke": 48},
+    "uint16": {"lists": LU, "lcb": 72, "lc": 48, "lie": 48, "lb": 30, "lpl": 24, "lpx": 24},
     F4: {"wq": 512, "uq": 128, "urq": 128, "vq": 128, "xq": C, "eq": 512, "nq": 512, "pq": C, "mq": A, "oq": C},
     U8: {"wp": 512, "up": 128, "urp": 128, "vp": 128, "xp": C, "ep": 512, "npl": 512, "pz": C, "mp": A, "op": C},
 }
 SCRATCH = {n: ("sbuf", [128, w], k) for k, m in WIDTHS.items() for n, w in m.items()}
+PART, _a = {}, 0
+for _s, _n in {"fc": 3, "ja": 32, "jb": 32, "jc": 32, "fr": 1, "da": 48, "db": 48, "dc": 48, "se": 24, "sm": 96, "sx": 96, "gg": 24, "sel": 192,
+               "seld": 96, "kf": 48, "kg": 48, "ks": 48, "kt": 48, "ls": 24, "pos": 24, "ps_": 64, "pr": 128}.items():
+    PART[_s] = (_a, _a + _n)
+    _a += _n
+SCRATCH["small"] = ("sbuf", [128, _a], "float32")
 SCRATCH["psA"] = SCRATCH["psB"] = ("psum", [128, 2048], "float32")
-GROUPS = {
-    "ic_": ("int32", {"pi": 1, "pm": 1, "pp": 1, "ia": 16, "ib": 16, "ic": 24, "i1": 30, "i2": 16, "i3": 24, "i8": 8, "i9": 8,
-                      "n1": 24, "n2": 24, "n3": 24, "i4": 64, "i5": 64, "k1": 48, "k2": 48, "k3": 48, "ke": 48}),
-    "fc_": ("float32", {"fm": 1, "f24": 1, "f32m": 1, "f16m": 1, "f16p": 1, "fr": 1, "w3": 64, "w4": 64, "w5": 64,
-                        "kf": 48, "kg": 48, "ks": 48, "sel1": 72, "sel2": 72, "seld": 72}),
-    "lk_": ("uint16", {"lnat": 24, "lback": 24, "lu": 8, "lcd": 48, "ly": 30, "ld": 24, "ltot": 8, "ldup": 16, "lc": 48}),
-}
-PART = {}
-for _g, (_k, _m) in GROUPS.items():
-    _a = 0
-    for _s, _n in _m.items():
-        PART[_s] = (_g, _a, _n)
-        _a += _n + _n % 2
-    SCRATCH[_g] = ("sbuf", [128, _a], _k)
 for _t in range(R + 1):
     SCRATCH["tq%d" % _t] = ("sbuf", [128, C], F4)
     SCRATCH["tp%d" % _t] = ("sbuf", [128, C], U8)
@@ -65,17 +72,18 @@ def rank_program(g, core, T, topo):
         if r[2] <= o[1] or o[2] <= r[1]: return True
         return r[3] > 1 and r[3] == o[3] and (r[1] - o[1]) % r[3] != 0
 
+    def psum(r): return r[0] in ("psA", "psB")
+
     def widen(r):
-        return (r[0], r[1] // 512 * 512, (r[2] + 511) // 512 * 512, 1) if r[0][:2] == "ps" else r
+        return (r[0], r[1] // 512 * 512, (r[2] + 511) // 512 * 512, 1) if psum(r) else r
 
     def settle(q, reads, writes):
         need = {}
         for w, rs in ((False, reads), (True, writes)):
             for r in rs:
-                bank = r[0][:2] == "ps"
                 for o in log.get(r[0], ()):
                     if apart(widen(r), o["r"]): continue
-                    if not (w or o["w"]) and not (bank and o["q"] != q): continue
+                    if not (w or o["w"]) and not (psum(r) and o["q"] != q): continue
                     need[o["n"]] = o
         for n in sorted(need, reverse=True):
             o = need[n]
@@ -102,10 +110,10 @@ def rank_program(g, core, T, topo):
         note(q, reads, writes, s, count[s])
 
     def B(name, a=0, b=None, step=1):
-        if name in PART:
-            p, o, n = PART[name]
-            return (p, o + a, o + (n if b is None else b), step)
-        return (name, a, SCRATCH[name][1][1] if b is None else b, step)
+        x, y = PART.get(name, (0, 0))
+        return ("small", x + a, y if b is None else x + b, step) if y else (name, a, SCRATCH[name][1][1] if b is None else b, step)
+
+    def L(name, buf="lists"): return B(buf, LAT[name][0], LAT[name][1])
 
     def ap(r):
         return T[r[0]][:, r[1]:r[2]] if r[3] == 1 else T[r[0]][:, r[1]:r[2]:r[3]]
@@ -127,16 +135,16 @@ def rank_program(g, core, T, topo):
     def mm(out, a, asc, b, bsc): run("t", lambda: g.tensor.matmul_mx(ap(out), ap(a), ap(asc), ap(b), ap(bsc), True, True), [a, asc, b, bsc], [out])
     def act(out, i): run("s", lambda: g.scalar.activation(ap(out), ap(i), AF.Copy), [i], [out])
     def actm(out, i, k): run("s", lambda: g.scalar.activation(ap(out), ap(i), AF.Copy, scale=k), [i], [out])
+    def acta(out, i, k): run("s", lambda: g.scalar.activation(ap(out), ap(i), AF.Identity, bias=k), [i], [out])
     def acti(out, i, off): run("s", lambda: g.scalar.activation(ap(out), ind(i, off), AF.Copy), [i, off], [out])
     def pick(q, p, i, ip, off):
         run("v", lambda: g.vector.tensor_copy(ap(q).bitcast(dt.uint32), ap(i).bitcast(dt.uint32).indirect(ap(off))), [i, off], [q])
         acti(p, ip, off)
     def iota(out, pattern, base, cm): run("g", lambda: g.iota(ap(out), pattern, base, cm), [], [out])
     def iotaf(out, pattern, base, cm): run("g", lambda: g.iota(ap(out), pattern, base, cm, allow_small_or_imprecise_dtypes=True), [], [out])
+    def keep(out, i, pattern, op, base, cm): run("g", lambda: g.affine_select(ap(out), ap(i), pattern, op, 0.0, base, cm), [i], [out])
     def units(name, ones):
-        for b in range(4):
-            o = B(name, 512 * b, 512 * b + 512)
-            run("g", lambda: g.affine_select(ap(o), ap(B(ones)), [[1, 512]], OP.is_equal, 0.0, -b, -4), [B(ones)], [o])
+        for b in range(4): keep(B(name, 512 * b, 512 * b + 512), B(ones), [[1, 512]], OP.is_equal, -b, -4)
     ndma = [0]
 
     def dma(pairs, reads, writes):
@@ -177,120 +185,101 @@ def rank_program(g, core, T, topo):
     dma([("s", T.vt[:, :], T.v[:, :])], [], [B("vt")])
 
     iota(B("pi"), [[0, 1]], 0, 1)
-    iota(B("ic"), [[1, 24]], 0, 0)
-    iota(B("i8"), [[16, 8]], 0, 0)
-    iota(B("ia"), [[1, 16]], 128, -1)
-    iota(B("ib"), [[1, 16]], 0, 0)
-    iota(B("i1"), [[1, 15], [256, 2]], 17, 0)
-    iota(B("i9"), [[24, 4], [0, 2]], 23, 0)
-    iota(B("i2"), [[32, 4], [0, 2], [16, 2]], 0, 0)
-    iota(B("i4"), [[0, 2], [1, 32]], 0, 0)
-    iota(B("i5"), [[1, 2], [0, 32]], 0, 0)
-    iota(B("i3"), [[16, 24]], 0, 0)
-    iotaf(B("i6"), [[1, 24], [32, 16]], 16, 0)
+    a = 0
+    while a < len(LISTS):
+        e = a
+        while e < len(LISTS) and LISTS[e][4] == LISTS[a][4]: e += 1
+        fill(B("lj", LAT[LISTS[a][0]][0], LAT[LISTS[e - 1][0]][1]), LISTS[a][4])
+        a = e
+    for s, n, p, b, k in LISTS: iota(L(s, "li"), p, b, 0)
+    fill(B("co", 0, 48), -767)
+    fill(B("co", 48, 72), -383)
+    iota(B("ia"), [[0, 48], [1, 16]], 128, -1)
     fill(B("one"), 1.0)
-    units("et", "one")
-    ts(B("pm"), B("pi"), 15, OP.bitwise_and)
-    copy(B("fm"), B("pm"))
-    ts(B("f24"), B("pm"), 24.0, OP.mult)
-    ts(B("lnat"), B("ic"), B("f24"), OP.add)
-    copy(B("lu"), B("i8"))
-    ts(B("ia"), B("ia"), 15, OP.bitwise_and)
-    ts(B("dg", 0, 16), B("ia"), 0.0, OP.is_equal)
-    ts(B("rs", 0, 16), B("ib"), 0.0, OP.is_gt)
-    ts(B("rq", 0, 24), B("ic"), 0.0, OP.is_gt)
-    for name, n, w in (("dg", 768, 16), ("rs", 1152, 16), ("rq", 96, 24)):
-        while w < n:
-            k = min(w, n - w)
-            copy(B(name, w, w + k), B(name, 0, k))
-            w += k
-    ts(B("n1"), B("ic"), B("f24"), OP.add)
-    ts(B("n2"), B("n1"), 15, OP.bitwise_and)
-    ts(B("n3"), B("n1"), 4, OP.arith_shift_right)
-    ts(B("n2"), B("n2"), 48.0, OP.mult)
-    tt(B("n2"), B("n2"), B("n3"), OP.add)
-    copy(B("lcd", 0, 24), B("n2"))
-    ts(B("lcd", 24, 48), B("n2"), 24.0, OP.add)
+    for k in range(3): keep(B("rs", 384 * k, 384 * k + 384), B("one", 0, 384), [[0, 24], [1, 16]], OP.not_equal, 0, 0)
+    for k, n in ((0, 15), (1, 31), (2, 16)): ts(B("pm", k, k + 1), B("pi"), n, OP.bitwise_and)
+    copy(B("fc"), B("pm"))
+    pm, pr, po = B("fc", 0, 1), B("fc", 1, 2), B("fc", 2, 3)
+    ts(B("lk"), B("lj"), pm, OP.mult)
+    tt(B("lk"), B("lk"), B("li"), OP.add)
+    copy(B("lists"), B("lk", 0, LU))
+    x = LAT["an"][0]
+    ts(B("lv"), B("lk", x, x + 72), 12, OP.arith_shift_right)
     quant(B("uq"), B("up"), B("ut"))
-    pick(B("urq"), B("urp"), B("uq"), B("up"), B("lu"))
-    fill(B("zero"), 0.0)
-    fill(B("onen"), -1.0)
+    tt(B("lw"), B("lv"), B("co"), OP.mult)
+    pick(B("urq"), B("urp"), B("uq"), B("up"), L("lu"))
+    tt(B("lx"), B("lw"), B("lk", x + 72, x + 144), OP.add)
+    ts(B("ia"), B("ia"), 15, OP.bitwise_and)
+    copy(B("lcb"), B("lx"))
+    ts(B("dg"), B("ia"), 0.0, OP.is_equal)
+    units("et", "one")
     fill(B("sb", C, PW), 0.0)
+    fill(B("onen"), -1.0)
+    fill(B("zero"), 0.0)
 
     def lists_of_candidates():
-        tti(B("c1", 0, 768), B("cdf"), B("lcd"), B("dg"), OP.mult)
+        tti(B("c1", 0, 768), B("cdf"), B("lcb", 0, 48), B("dg"), OP.mult)
         scan(B("c2", 0, 768), B("rs", 0, 768), B("c1", 0, 768))
-        copy(B("k1"), B("c2", 15, 768, 16))
-        ts(B("k2"), B("k1"), 2731.0, OP.mult)
-        ts(B("k2"), B("k2"), 16, OP.arith_shift_right)
+        ts(B("k1"), B("c2", 15, 768, 16), 171.0, OP.mult)
+        ts(B("k3"), B("c2", 15, 768, 16), 16.0, OP.mult)
+        ts(B("k2"), B("k1"), 12, OP.arith_shift_right)
+        ts(B("fr"), pm, 0.0, OP.is_equal, 385.0, OP.mult)
         ts(B("k2"), B("k2"), -383.0, OP.mult)
-        ts(B("k3"), B("k1"), 16.0, OP.mult)
         tt(B("ke"), B("k2"), B("k3"), OP.add)
-        ts(B("fr"), B("fm"), 0.0, OP.is_equal, 385.0, OP.mult)
-        for h in (0, 24): tt(B("ke", h, h + 1), B("ke", h, h + 1), B("fr"), OP.add)
+        ts(B("ke", 0, 2), B("ke", 0, 2), B("fr"), OP.add)
         copy(B("lc"), B("ke"))
 
     def lists_inside():
         ts(B("k2"), B("ke"), 15, OP.bitwise_and)
-        ts(B("kf"), B("k2"), B("fm"), OP.is_equal)
-        ts(B("kg"), B("kf"), -1.0, OP.mult, 1.0, OP.add)
-        ts(B("ks"), B("ke"), -386.0, OP.add)
+        tt(B("sel", 96, 144), B("ke"), L("ep", "lk"), OP.is_equal)
+        ts(B("kt"), B("ke"), -1.0, OP.mult, 386.0, OP.add)
+        ts(B("kf"), B("k2"), pm, OP.is_equal)
         ts(B("k3"), B("ke"), 16.0, OP.add)
-        for h, s in ((0, "sel1"), (24, "sel2")):
-            copy(B(s, 0, 24), B("ke", h, h + 24))
-            tt(B(s, 24, 48), B("k3", h, h + 24), B("kf", h, h + 24), OP.mult)
-            tt(B(s, 48, 72), B("ks", h, h + 24), B("kg", h, h + 24), OP.mult)
-            ts(B(s, 48, 72), B(s, 48, 72), 386.0, OP.add)
-        tt(B("seld"), B("sel2"), B("sel1"), OP.subtract)
+        tt(B("kg"), B("kf"), B("sel", 96, 144), OP.subtract)
+        tt(B("kt"), B("kt"), B("kf"), OP.mult)
+        ts(B("ks"), B("sel", 96, 144), 14.0, OP.mult)
+        tt(B("sel", 0, 48), B("kg"), B("k3"), OP.mult)
+        tt(B("kt"), B("kt"), B("ke"), OP.add)
+        ts(B("sel", 144, 192), B("ke"), -float(C), OP.add)
+        tt(B("sel", 48, 96), B("kt"), B("ks"), OP.add)
+        tt(B("seld"), B("sel", 1, 192, 2), B("sel", 0, 192, 2), OP.subtract)
 
     def table():
+        iotaf(B("i6"), [[1, 24], [32, 16]], 16, 0)
+        fill(B("tbl", C, 400), 0.0)
+        fill(B("tbl", 386, 387), UNIT)
+        acta(B("tbl", 0, C), B("i6"), UNIT)
+        acta(B("tbl", 400, 800), B("tbl", 0, 400), UNIT)
+        iota(B("jj"), [[1, 32]], 0, 0)
         iotaf(B("jid"), [[1, C]], -192, 0)
+        keep(B("rq"), B("one", 0, 128), [[0, 4], [1, 32]], OP.not_equal, 0, 0)
+        keep(B("r5"), B("one", 0, 120), [[0, 24], [1, 5]], OP.not_equal, 0, 0)
+        iotaf(B("cls"), [[1, 4], [0, 32]], 0, 0)
         units("en", "onen")
-        fill(B("tbl", C, PW), 0.0)
-        fill(B("tbl", 386, 387), 0.0009765625)
-        run("s", lambda: g.scalar.activation(ap(B("tbl", 0, C)), ap(B("i6")), AF.Identity, bias=0.0009765625), [B("i6")], [B("tbl", 0, C)])
 
     def late_constants():
         fill(B("y1", 0, 16), 0.0)
         fill(B("y1", 400, YW), 0.0)
         fill(B("d2", 0, 16), 0.0)
-        ts(B("f16m"), B("pm"), 16.0, OP.mult)
-        ts(B("f32m"), B("pm"), 32.0, OP.mult)
-        ts(B("ly"), B("i1"), B("f16m"), OP.add)
-        ts(B("ld"), B("ic"), B("f32m"), OP.add, 16.0, OP.add)
-        copy(B("ltot"), B("i9"))
-        ts(B("ldup"), B("i2"), B("fm"), OP.add)
-        ts(B("pp"), B("pi"), 4, OP.arith_shift_right, 1, OP.bitwise_and)
-        ts(B("f16p"), B("pp"), 16.0, OP.mult)
-        ts(B("w4"), B("i4"), B("f16p"), OP.subtract)
-        ts(B("w5"), B("w4"), B("fm"), OP.is_lt)
-        tt(B("w5"), B("w5"), B("i5"), OP.not_equal)
-        ts(B("w3"), B("w4"), 0.0, OP.is_ge)
-        tt(B("w5"), B("w5"), B("w3"), OP.mult)
-        ts(B("w3"), B("w4"), 15.0, OP.is_le)
-        tt(B("mk", 0, 64), B("w5"), B("w3"), OP.mult)
+        fill(B("own", 0, 16), 0.0)
+        fill(B("w2"), 1.0)
+        fill(B("dm"), 9.0)
+        ts(B("ja"), B("jj"), po, OP.subtract, 0.0, OP.is_ge)
+        ts(B("jb"), B("jj"), pr, OP.subtract, 0.0, OP.is_ge)
+        ts(B("jc"), B("jj"), po, OP.subtract, 16.0, OP.is_ge)
+        tt(B("mk", 0, 32), B("ja"), B("jb"), OP.subtract)
+        tt(B("mk", 32, 64), B("jb"), B("jc"), OP.subtract)
         copy(B("mk", 64, 128), B("mk", 0, 64))
         copy(B("mk", 128, 256), B("mk", 0, 128))
-        fill(B("w2"), 1.0)
         for b in range(4):
             for name in ("fn", "ma", "mb", "mc"): act(B(name, PW * b + C, PW * b + PW), B("zero"))
             act(B("rp", RW * b + A, RW * b + RW), B("zero"))
-
-    def last_constants():
-        ts(B("n1"), B("i3"), B("fm"), OP.add)
-        ts(B("n2"), B("n1"), 2731.0, OP.mult)
-        ts(B("n2"), B("n2"), 16, OP.arith_shift_right)
-        ts(B("n2"), B("n2"), -383.0, OP.mult)
-        ts(B("n3"), B("n1"), 16.0, OP.mult)
-        tt(B("n3"), B("n2"), B("n3"), OP.add)
-        copy(B("lback"), B("n3"))
-        quant(B("vq"), B("vp"), B("vt"))
 
     for t in range(R):
         tq, tp, aq, apl, al, ao = ["%s%d" % (s, t) for s in ("tq", "tp", "aq", "ap", "al", "ao")]
         if t == 0:
             quant(B("xq"), B("xp"), B("xt0"))
-            pick(B(tq), B(tp), B("xq"), B("xp"), B("lnat"))
+            pick(B(tq), B(tp), B("xq"), B("xp"), L("lnat"))
         else:
             for h in (0, 192): quant(B(tq, h, h + 192), B(tp, h, h + 192), B("xt", 4 * h, 4 * h + 768))
         for h, k in ((0, 0), (192, 512)):
@@ -301,65 +290,67 @@ def rank_program(g, core, T, topo):
         if t == 0:
             lists_of_candidates()
             table()
+        tt(B("c1", 768, 960), B("psA", 0, 192), B("dg", 0, 192), OP.mult)
         tti(B("c1", 0, 768), B("sb"), B("lc"), B("dg"), OP.mult)
-        for h, k in ((0, 0), (192, 512)): tt(B("c1", 768 + h, 960 + h), B("psA", k, k + 192), B("dg", 0, 192), OP.mult)
+        tt(B("c1", 960, 1152), B("psA", 512, 704), B("dg", 0, 192), OP.mult)
         scan(B("c2"), B("rs"), B("c1"))
         if t == 0:
             lists_inside()
             quant(B("eq"), B("ep"), B("et"))
-        for h in (0, 24): tt(B("da", h, h + 24), B("c2", 16 * h + 15, 16 * h + 384, 16), B("c2", 783, 1152, 16), OP.subtract)
-        ts(B("db"), B("da"), -1.0, OP.mult)
+        for h in (0, 1): tt(B("da", 24 * h, 24 * h + 24), B("c2", 16 * h + 15, 768, 32), B("c2", 783, 1152, 16), OP.subtract)
+        for h in (0, 1): tt(B("db", 24 * h, 24 * h + 24), B("c2", 783, 1152, 16), B("c2", 16 * h + 15, 768, 32), OP.subtract)
         tt(B("dc"), B("da"), B("db"), OP.max)
         tt(B("se"), B("dc", 24, 48), B("dc", 0, 24), OP.is_lt)
-        for h in (48, 24, 0): tt(B("sm", h, h + 24), B("seld", h, h + 24), B("se"), OP.mult)
-        tt(B("sx"), B("sm"), B("sel1"), OP.add)
-        copy(B("lex"), B("sx", 48, 72))
-        copy(B("lin", 0, 48, 2), B("sx", 24, 48))
-        ts(B("bz"), B("sx", 0, 24), -float(C), OP.add)
-        acti(B("own", 0, 64), B("tbl"), B("lex", 0, 4))
-        acti(B("own", 64, C), B("tbl"), B("lex", 4, 24))
+        for h in (0, 24, 48): tt(B("sm", h, h + 24), B("seld", h, h + 24), B("se"), OP.mult)
+        tt(B("sx", 0, 72), B("sm", 0, 72), B("sel", 0, 144, 2), OP.add)
+        tt(B("sm", 72, 96), B("seld", 72, 96), B("se"), OP.mult)
+        for h in (0, 12): tt(B("gg", h, h + 12), B("sx", 49, 72, 2), B("sx", 2 * h, 2 * h + 24, 2), OP.mult)
+        tt(B("sx", 72, 96), B("sm", 72, 96), B("sel", 144, 192, 2), OP.add)
+        tt(B("sx", 1, 48, 2), B("sx", 1, 48, 2), B("gg"), OP.add)
+        copy(B("lie"), B("sx", 0, 48))
+        if t == 0: late_constants()
+        for x, y in ((0, 4), (4, 10), (10, 24)): acti(B("own", 16 + 16 * x, 16 + 16 * y), B("tbl"), B("lie", 24 + x, 24 + y))
         for b in range(4):
             mm(B("psB", 512 * b, 512 * b + C), side("eq", b), side("ep", b), B(tq), B(tp))
             act(body("fp", b), B("psB", 512 * b, 512 * b + C))
-        if t == 0: late_constants()
-        copy(B("y1", 16, 32), B("own", 0, 16))
-        for q in range(1, Q):
-            tti(B("y1", 16 + 16 * q, 32 + 16 * q), B("y1", 0, 16 + 16 * q), B("lin", 2 * q, 2 * q + 1), B("own", 16 * q, 16 * q + 16), OP.add)
-        if t == 0: quant(B("nq"), B("npl"), B("en"))
-        tti(B("c1", 0, 480), B("y1"), B("ly"), B("dg", 0, 480), OP.mult)
-        scan(B("c2", 0, 480), B("rs", 0, 480), B("c1", 0, 480))
-        copy(B("lb"), B("c2", 15, 480, 16))
+        for k in range(32, C, 32):
+            tti(B("y1", 16 + k, 48 + k), B("own" if k == 32 else "y1", 0, 16 + k), B("lie", k // 16, k // 16 + 2), B("own", 16 + k, 48 + k), OP.add)
+            if k == 32: copy(B("y1", 16, 48), B("own", 16, 48))
+        tti(B("c1", 0, 480), B("y1"), L("ly"), B("dg", 0, 480), OP.mult)
         copy(B("d2", 16, 48), B("y1", 16, YW, 16))
+        scan(B("c2", 0, 480), B("rs", 0, 480), B("c1", 0, 480))
+        if t == 0: quant(B("nq"), B("npl"), B("en"))
+        copy(B("lb"), B("c2", 15, 480, 16))
         for m in range(1, M):
             tti(B("d2", 16 + 32 * m, 48 + 32 * m), B("d2", 0, 16 + 32 * m), B("lb", 2 * m - 2, 2 * m), B("y1", 16 + m, YW, 16), OP.add)
-        tti(B("c1", 0, C), B("d2"), B("ld"), B("dg", 0, C), OP.mult)
+        tti(B("c1", 0, C), B("d2"), L("ld"), B("dg", 0, C), OP.mult)
         scan(B("c2", 0, C), B("rs", 0, C), B("c1", 0, C))
-        ts(B("dw"), B("c2", 15, C, 16), 1024.0, OP.mult)
-        ts(B("dm"), B("dw"), 3, OP.bitwise_and)
-        ts(B("pos"), B("dm"), 0.0, OP.is_gt)
-        tt(B("ls", 0, 24), B("bz"), B("pos"), OP.mult)
-        ts(B("ql%d" % t), B("ls", 0, 24), float(C), OP.add)
-        send(2, t)
-        for c in range(4): ts(B("ind", 24 * c, 24 * c + 24), B("dm"), float(c), OP.is_equal)
+        ts(B("dw"), B("c2", 15, C, 16), 1 / UNIT, OP.mult)
+        ts(B("dm", 0, 24), B("dw"), 3, OP.bitwise_and)
+        ts(B("pos"), B("dm", 0, 24), 0.0, OP.is_gt)
+        tti(B("ind"), B("dm"), L("lcls"), B("cls"), OP.is_equal)
+        tt(B("ls"), B("sx", 72, 96), B("pos"), OP.mult)
         scan(B("inc"), B("rq"), B("ind"))
-        copyi(B("tb"), B("inc"), B("ltot"))
+        ts(B("ql%d" % t), B("ls"), float(C), OP.add)
+        send(2, t)
+        copyi(B("tb"), B("inc"), L("ltot"))
+        tt(B("pr"), B("ind"), B("inc"), OP.mult)
         run("v", lambda: g.vector.transpose(ap(B("tv")), ap(B("tb"))), [B("tb")], [B("tv")])
-        tti(B("w1"), B("tv"), B("ldup"), B("mk"), OP.mult)
+        tt(B("ps_"), B("pr", 0, 64), B("pr", 64, 128), OP.add)
+        tti(B("w1"), B("tv"), L("ldup"), B("mk"), OP.mult)
+        tt(B("pu", 4, 120, 5), B("ps_", 0, 24), B("ps_", 32, 56), OP.add)
         scan(B("bs"), B("w2"), B("w1"))
-        for c in range(4): ts(B("pu", 24 * c, 24 * c + 24), B("inc", 24 * c, 24 * c + 24), B("bs", 64 * c + 31, 64 * c + 32), OP.add, -1.0, OP.add)
-        tt(B("ls"), B("pu"), B("ind"), OP.mult)
-        tt(B("pu", 0, 48), B("ls", 0, 48), B("ls", 48, 96), OP.add)
-        tt(B("pl"), B("pu", 0, 24), B("pu", 24, 48), OP.add)
-        copy(B("lpl"), B("pl"))
+        for c in range(4): ts(B("pu", c, 120, 5), B("ind", 32 * c, 32 * c + 24), B("bs", 64 * c + 31, 64 * c + 32), OP.mult)
+        scan(B("pv"), B("r5"), B("pu"))
+        ts(B("lpl"), B("pv", 4, 120, 5), -1.0, OP.add)
+        ts(B("lpx"), B("pv", 4, 120, 5), -1.0, OP.add, float(A), OP.min)
         run("v", lambda: g.vector.tensor_copy(ind(B("of"), B("lpl")), ap(B("jid"))), [B("jid"), B("lpl")], [B("of")])
-        ts(B("lpx"), B("pl"), float(A), OP.min)
         for k in range(4): expect(k, t)
         for b in range(4):
             mm(B("psA", 512 * b, 512 * b + C), side("nq", b), side("npl", b), B(aq), B(apl))
-            act(body("fn", b), B("psA", 512 * b, 512 * b + C))
-            act(body("fm2", b), B("psA", 512 * b, 512 * b + C))
+            for name in ("fn", "fo"): act(body(name, b), B("psA", 512 * b, 512 * b + C))
         for b in range(4):
-            tti(B("pt", b, 4 * C, 4), plane("fn", b), B(al), body("fm2", b), OP.subtract)
+            tti(B("pt", b, 4 * C, 4), plane("fn", b), B(al), body("fo", b), OP.subtract)
         for h, ps in ((0, "psB"), (192, "psA")):
             quant(B("pq", h, h + 192), B("pz", h, h + 192), B("pt", 4 * h, 4 * h + 768))
             mm(B(ps, 0, 192), side("eq", 0), side("ep", 0), B("pq", h, h + 192), B("pz", h, h + 192))
@@ -372,17 +363,16 @@ def rank_program(g, core, T, topo):
         scan(B("oh"), B("rs", 0, A), B("og"))
         ts(B("qo%d" % t), B("oh", 15, A, 16), 192.0, OP.add)
         send(3, t)
-        for b in range(4):
-            for src, dst in (("ma", "mb"), ("mb", "mc"), ("mc", "mb")):
-                tti(body(dst, b), plane(src, b), B(al), body("md", b), OP.add)
-            if b < 3: acti(B("mt", b, 4 * A, 4), plane("mb", b), B(ao))
+        for src, dst in (("ma", "mb"), ("mb", "mc"), ("mc", "mb")):
+            for b in range(4): tti(body(dst, b), plane(src, b), B(al), body("md", b), OP.add)
+        for b in range(3): acti(B("mt", b, 4 * A, 4), plane("mb", b), B(ao))
         acti(B("mt", 3, 640, 4), plane("mb", 3), B(ao, 0, 10))
         copyi(B("mt", 643, 1280, 4), plane("mb", 3), B(ao, 10, 20))
         for h, ps in ((0, "psA"), (160, "psB")):
             quant(B("mq", h, h + 160), B("mp", h, h + 160), B("mt", 4 * h, 4 * h + 640))
             mm(B(ps, 0, 160), side("wq", 0), side("wp", 0), B("mq", h, h + 160), B("mp", h, h + 160))
             actm(B("rp", h, h + 160), B(ps, 0, 160), 0.015625)
-        if t == R - 1: last_constants()
+        if t == R - 1: quant(B("vq"), B("vp"), B("vt"))
         for b in range(1, 4):
             mm(B("psA", 512 * b, 512 * b + A), side("wq", b), side("wp", b), B("mq"), B("mp"))
             actm(B("rp", RW * b, RW * b + A), B("psA", 512 * b, 512 * b + A), 0.015625)
@@ -390,7 +380,7 @@ def rank_program(g, core, T, topo):
             tti(B("xt", b, 4 * C, 4), B("rp", RW * b, RW * b + RW), B("lpx"), body("fp", b), OP.add)
 
     quant(B("tq%d" % R), B("tp%d" % R), B("xt"))
-    pick(B("oq"), B("op"), B("tq%d" % R), B("tp%d" % R), B("lback"))
+    pick(B("oq"), B("op"), B("tq%d" % R), B("tp%d" % R), B("lcb", 48, 72))
     dma([("y", T.oc[:, :], T.oq[:, :].bitcast(dt.uint8))], [B("oq")], [])
     dma([("s", T.osc[4 * k:4 * k + 4, :], T.op[32 * k:32 * k + 4, :]) for k in range(4)], [B("op")], [])
     mm(B("psB", 0, C), B("vq"), B("vp"), B("oq"), B("op"))

@@ -11,8 +11,6 @@ F4, U8 = "float8_e4m3fn_x4", "uint8"
 
 LISTS = [("lnat", 24, [[1, 24]], 0, 24),
          ("lu", 8, [[16, 8]], 0, 0), ("ltot", 8, [[32, 4], [0, 2]], 31, 0),
-         ("ly", 30, [[1, 15], [256, 2]], 17, 16),
-         ("ld", 24, [[1, 24]], 16, 32),
          ("ldup", 16, [[32, 4], [0, 2], [16, 2]], 0, 1), ("lcls", 8, [[0, 4], [16, 2]], 0, 1),
          ("an", 48, [[256, 24], [0, 2]], 0, 6144), ("al", 24, [[2736, 24]], 0, 171),
          ("bn", 48, [[48, 24], [24, 2]], 0, 1152), ("bl", 24, [[256, 24]], 0, 16),
@@ -26,8 +24,8 @@ LW, LU = _a, LAT["an"][0]
 WIDTHS = {
     "bfloat16": {"xt0": 4 * C, "ut": 512, "vt": 512, "one": 512, "onen": 512, "et": 2048, "en": 2048, "dg": 768, "rs": 1152, "rq": 128, "r5": 120,
                  "mk": 256, "jid": C, "tb": 128, "tv": 128, "of": C, "og": A, "oh": A, "fp": 4 * PW, "fn": 4 * PW, "fo": 4 * PW,
-                 "pt": 4 * C, "ma": 4 * PW, "mb": 4 * PW, "mc": 4 * PW, "md": 4 * PW, "mt": 4 * A, "xt": 4 * C},
-    "float32": {"zero": 16, "w1": 256, "w2": 256, "tbl": 800, "i6": C, "cls": 128, "sb": PW, "c1": 1152, "c2": 1152,
+                 "pt": 4 * C, "ma": 4 * PW, "mb": 4 * PW, "mc": 4 * PW, "mg": 4 * PW, "md": 4 * PW, "mt": 4 * A, "xt": 4 * C},
+    "float32": {"zero": 16, "w1": 256, "w2": 256, "tbl": 800, "i6": C, "cls": 128, "sb": PW, "c1": 1152, "c2": 1152, "e1": 480, "e2": C,
                 "own": 16 + C, "y1": YW, "d2": YW, "ind": 128, "inc": 128, "bs": 256, "pu": 120, "pv": 120, "rp": 4 * RW, "yo": C},
     "int32": {"cdf": 768, "dw": 24, "dm": 32, "pi": 1, "pm": 3, "ia": 768, "jj": 32, "li": LW, "lj": LW, "lk": LW, "lv": 72, "lw": 72, "lx": 72, "co": 72,
               "k1": 48, "k2": 48, "k3": 48, "ke": 48},
@@ -258,22 +256,28 @@ def rank_program(g, core, T, topo):
         units("en", "onen")
 
     def late_constants():
+        fill(B("own", 0, 16), 0.0)
         fill(B("y1", 0, 16), 0.0)
         fill(B("y1", 400, YW), 0.0)
-        fill(B("d2", 0, 16), 0.0)
-        fill(B("own", 0, 16), 0.0)
-        fill(B("w2"), 1.0)
-        fill(B("dm"), 9.0)
-        ts(B("ja"), B("jj"), po, OP.subtract, 0.0, OP.is_ge)
-        ts(B("jb"), B("jj"), pr, OP.subtract, 0.0, OP.is_ge)
-        ts(B("jc"), B("jj"), po, OP.subtract, 16.0, OP.is_ge)
-        tt(B("mk", 0, 32), B("ja"), B("jb"), OP.subtract)
-        tt(B("mk", 32, 64), B("jb"), B("jc"), OP.subtract)
-        copy(B("mk", 64, 128), B("mk", 0, 64))
-        copy(B("mk", 128, 256), B("mk", 0, 128))
+        fill(B("e1"), 0.0)
         for b in range(4):
             for name in ("fn", "ma", "mb", "mc"): act(B(name, PW * b + C, PW * b + PW), B("zero"))
             act(B("rp", RW * b + A, RW * b + RW), B("zero"))
+        return [lambda: fill(B("d2", 0, 16), 0.0), lambda: fill(B("dm"), 9.0), lambda: fill(B("w2"), 1.0),
+                lambda: ts(B("ja"), B("jj"), po, OP.subtract, 0.0, OP.is_ge),
+                lambda: ts(B("jb"), B("jj"), pr, OP.subtract, 0.0, OP.is_ge),
+                lambda: ts(B("jc"), B("jj"), po, OP.subtract, 16.0, OP.is_ge),
+                lambda: tt(B("mk", 0, 32), B("ja"), B("jb"), OP.subtract),
+                lambda: tt(B("mk", 32, 64), B("jb"), B("jc"), OP.subtract),
+                lambda: copy(B("mk", 64, 128), B("mk", 0, 64)),
+                lambda: copy(B("mk", 128, 256), B("mk", 0, 128)),
+                lambda: quant(B("nq"), B("npl"), B("en"))]
+
+    def leave(k):
+        for q in (k // 16, k // 16 + 1): ts(B("e1", q, 480, 32), B("y1", 17 + 16 * q, 32 + 16 * q), B("dg", q % 16, q % 16 + 1), OP.mult)
+
+    def settled(m):
+        ts(B("e2", m, C, 16), B("d2", 16 + 32 * m, 40 + 32 * m), B("dg", m, m + 1), OP.mult)
 
     for t in range(R):
         tq, tp, aq, apl, al, ao = ["%s%d" % (s, t) for s in ("tq", "tp", "aq", "ap", "al", "ao")]
@@ -294,9 +298,7 @@ def rank_program(g, core, T, topo):
         tti(B("c1", 0, 768), B("sb"), B("lc"), B("dg"), OP.mult)
         tt(B("c1", 960, 1152), B("psA", 512, 704), B("dg", 0, 192), OP.mult)
         scan(B("c2"), B("rs"), B("c1"))
-        if t == 0:
-            lists_inside()
-            quant(B("eq"), B("ep"), B("et"))
+        if t == 0: lists_inside()
         for h in (0, 1): tt(B("da", 24 * h, 24 * h + 24), B("c2", 16 * h + 15, 768, 32), B("c2", 783, 1152, 16), OP.subtract)
         for h in (0, 1): tt(B("db", 24 * h, 24 * h + 24), B("c2", 783, 1152, 16), B("c2", 16 * h + 15, 768, 32), OP.subtract)
         tt(B("dc"), B("da"), B("db"), OP.max)
@@ -308,7 +310,8 @@ def rank_program(g, core, T, topo):
         tt(B("sx", 72, 96), B("sm", 72, 96), B("sel", 144, 192, 2), OP.add)
         tt(B("sx", 1, 48, 2), B("sx", 1, 48, 2), B("gg"), OP.add)
         copy(B("lie"), B("sx", 0, 48))
-        if t == 0: late_constants()
+        spare = late_constants() if t == 0 else []
+        if t == 0: quant(B("eq"), B("ep"), B("et"))
         for x, y in ((0, 4), (4, 10), (10, 24)): acti(B("own", 16 + 16 * x, 16 + 16 * y), B("tbl"), B("lie", 24 + x, 24 + y))
         for b in range(4):
             mm(B("psB", 512 * b, 512 * b + C), side("eq", b), side("ep", b), B(tq), B(tp))
@@ -316,15 +319,21 @@ def rank_program(g, core, T, topo):
         for k in range(32, C, 32):
             tti(B("y1", 16 + k, 48 + k), B("own" if k == 32 else "y1", 0, 16 + k), B("lie", k // 16, k // 16 + 2), B("own", 16 + k, 48 + k), OP.add)
             if k == 32: copy(B("y1", 16, 48), B("own", 16, 48))
-        tti(B("c1", 0, 480), B("y1"), L("ly"), B("dg", 0, 480), OP.mult)
+            else: leave(k - 64)
+            for f in spare[:2]: f()
+            spare = spare[2:]
+        leave(C - 64)
+        leave(C - 32)
+        scan(B("c2", 0, 480), B("rs", 0, 480), B("e1"))
         copy(B("d2", 16, 48), B("y1", 16, YW, 16))
-        scan(B("c2", 0, 480), B("rs", 0, 480), B("c1", 0, 480))
-        if t == 0: quant(B("nq"), B("npl"), B("en"))
         copy(B("lb"), B("c2", 15, 480, 16))
         for m in range(1, M):
             tti(B("d2", 16 + 32 * m, 48 + 32 * m), B("d2", 0, 16 + 32 * m), B("lb", 2 * m - 2, 2 * m), B("y1", 16 + m, YW, 16), OP.add)
-        tti(B("c1", 0, C), B("d2"), L("ld"), B("dg", 0, C), OP.mult)
-        scan(B("c2", 0, C), B("rs", 0, C), B("c1", 0, C))
+            settled(m - 1)
+            for f in spare[:1]: f()
+            spare = spare[1:]
+        settled(M - 1)
+        scan(B("c2", 0, C), B("rs", 0, C), B("e2"))
         ts(B("dw"), B("c2", 15, C, 16), 1 / UNIT, OP.mult)
         ts(B("dm", 0, 24), B("dw"), 3, OP.bitwise_and)
         ts(B("pos"), B("dm", 0, 24), 0.0, OP.is_gt)
@@ -344,27 +353,36 @@ def rank_program(g, core, T, topo):
         scan(B("pv"), B("r5"), B("pu"))
         ts(B("lpl"), B("pv", 4, 120, 5), -1.0, OP.add)
         ts(B("lpx"), B("pv", 4, 120, 5), -1.0, OP.add, float(A), OP.min)
-        run("v", lambda: g.vector.tensor_copy(ind(B("of"), B("lpl")), ap(B("jid"))), [B("jid"), B("lpl")], [B("of")])
         for k in range(4): expect(k, t)
         for b in range(4):
             mm(B("psA", 512 * b, 512 * b + C), side("nq", b), side("npl", b), B(aq), B(apl))
-            for name in ("fn", "fo"): act(body(name, b), B("psA", 512 * b, 512 * b + C))
-        for b in range(4):
-            tti(B("pt", b, 4 * C, 4), plane("fn", b), B(al), body("fo", b), OP.subtract)
+            for name in ("fn", "fo")[:1 + (b < 2)]: act(body(name, b), B("psA", 512 * b, 512 * b + C))
+        for b in (2, 3): acti(body("mg", b), plane("fn", b), B(al))
+        for b in (0, 1): tti(B("pt", b, 4 * C, 4), plane("fn", b), B(al), body("fo", b), OP.subtract)
+        for b in (2, 3): tt(B("pt", b, 4 * C, 4), body("mg", b), B("psA", 512 * b, 512 * b + C), OP.subtract)
         for h, ps in ((0, "psB"), (192, "psA")):
             quant(B("pq", h, h + 192), B("pz", h, h + 192), B("pt", 4 * h, 4 * h + 768))
             mm(B(ps, 0, 192), side("eq", 0), side("ep", 0), B("pq", h, h + 192), B("pz", h, h + 192))
             act(B("ma", h, h + 192), B(ps, 0, 192))
-        for h, ps in ((0, "psB"), (192, "psA")): act(B("md", h, h + 192), B(ps, 0, 192))
         for b in range(1, 4):
             mm(B("psB", 512 * b, 512 * b + C), side("eq", b), side("ep", b), B("pq"), B("pz"))
-            for name in ("ma", "md"): act(body(name, b), B("psB", 512 * b, 512 * b + C))
-        tt(B("og"), B("of", 0, A), B("dg", 0, A), OP.mult)
-        scan(B("oh"), B("rs", 0, A), B("og"))
-        ts(B("qo%d" % t), B("oh", 15, A, 16), 192.0, OP.add)
-        send(3, t)
+            act(body("ma", b), B("psB", 512 * b, 512 * b + C))
+            if b > 1: acti(body("mg", b), plane("ma", b), B(al))
+        run("v", lambda: g.vector.tensor_copy(ind(B("of"), B("lpl")), ap(B("jid"))), [B("jid"), B("lpl")], [B("of")])
+        order = [lambda: tt(B("og"), B("of", 0, A), B("dg", 0, A), OP.mult), lambda: scan(B("oh"), B("rs", 0, A), B("og")),
+                 lambda: ts(B("qo%d" % t), B("oh", 15, A, 16), 192.0, OP.add)]
         for src, dst in (("ma", "mb"), ("mb", "mc"), ("mc", "mb")):
-            for b in range(4): tti(body(dst, b), plane(src, b), B(al), body("md", b), OP.add)
+            if src != "ma":
+                for b in (2, 3): acti(body("mg", b), plane(src, b), B(al))
+            for b in (0, 1):
+                if src == "ma":
+                    order[b]()
+                    copy(body("md", b), body("ma", b))
+                tti(body(dst, b), plane(src, b), B(al), body("md", b), OP.add)
+            if src == "ma":
+                order[2]()
+                send(3, t)
+            for b in (2, 3): tt(body(dst, b), body("mg", b), B("psB", 512 * b, 512 * b + C), OP.add)
         for b in range(3): acti(B("mt", b, 4 * A, 4), plane("mb", b), B(ao))
         acti(B("mt", 3, 640, 4), plane("mb", 3), B(ao, 0, 10))
         copyi(B("mt", 643, 1280, 4), plane("mb", 3), B(ao, 10, 20))

from concourse.mybir import dt, AluOpType, ActivationFunctionType

C, A, R, N = 384, 320, 3, 8
STEP = [1, 2, 4]
Q, M = 24, 16
PW = 400
RW = 336
YW = 528
UNIT = 0.0009765625
F4, U8 = "float8_e4m3fn_x4", "uint8"

LISTS = [("lnat", 24, [[1, 24]], 0, 24),
         ("lu", 8, [[16, 8]], 0, 0), ("ltot", 8, [[32, 4], [0, 2]], 31, 0),
         ("ldup", 16, [[32, 4], [0, 2], [16, 2]], 0, 1), ("lcls", 8, [[0, 4], [16, 2]], 0, 1),
         ("an", 48, [[256, 24], [0, 2]], 0, 6144), ("al", 24, [[2736, 24]], 0, 171),
         ("bn", 48, [[48, 24], [24, 2]], 0, 1152), ("bl", 24, [[256, 24]], 0, 16),
         ("ep", 48, [[32, 12], [1000, 2], [0, 2]], -1000, 1)]
LAT, _a = {}, 0
for _s, _n, _p, _b, _k in LISTS:
    LAT[_s] = (_a, _a + _n)
    _a += _n
LW, LU = _a, LAT["an"][0]

WIDTHS = {
    "bfloat16": {"xt0": 4 * C, "ut": 512, "vt": 512, "one": 512, "onen": 512, "et": 2048, "en": 2048, "dg": 768, "rs": 1152, "rq": 128, "r5": 120,
                 "mk": 256, "jid": C, "tb": 128, "tv": 128, "of": C, "og": A, "oh": A, "fp": 4 * PW, "fn": 4 * PW, "fo": 4 * PW,
                 "pt": 4 * C, "ma": 4 * PW, "mb": 4 * PW, "mc": 4 * PW, "mg": 4 * PW, "md": 4 * PW, "mt": 4 * A, "xt": 4 * C},
    "float32": {"zero": 16, "w1": 256, "w2": 256, "tbl": 800, "i6": C, "cls": 128, "sb": PW, "c1": 1152, "c2": 1152, "e1": 480, "e2": C,
                "own": 16 + C, "y1": YW, "d2": YW, "ind": 128, "inc": 128, "bs": 256, "pu": 120, "pv": 120, "rp": 4 * RW, "yo": C},
    "int32": {"cdf": 768, "dw": 24, "dm": 32, "pi": 1, "pm": 3, "ia": 768, "jj": 32, "li": LW, "lj": LW, "lk": LW, "lv": 72, "lw": 72, "lx": 72, "co": 72,
              "k1": 48, "k2": 48, "k3": 48, "ke": 48},
    "uint16": {"lists": LU, "lcb": 72, "lc": 48, "lie": 48, "lb": 30, "lpl": 24, "lpx": 24},
    F4: {"wq": 512, "uq": 128, "urq": 128, "vq": 128, "xq": C, "eq": 512, "nq": 512, "pq": C, "mq": A, "oq": C},
    U8: {"wp": 512, "up": 128, "urp": 128, "vp": 128, "xp": C, "ep": 512, "npl": 512, "pz": C, "mp": A, "op": C},
}
SCRATCH = {n: ("sbuf", [128, w], k) for k, m in WIDTHS.items() for n, w in m.items()}
PART, _a = {}, 0
for _s, _n in {"fc": 3, "ja": 32, "jb": 32, "jc": 32, "fr": 1, "da": 48, "db": 48, "dc": 48, "se": 24, "sm": 96, "sx": 96, "gg": 24, "sel": 192,
               "seld": 96, "kf": 48, "kg": 48, "ks": 48, "kt": 48, "ls": 24, "pos": 24, "ps_": 64, "pr": 128}.items():
    PART[_s] = (_a, _a + _n)
    _a += _n
SCRATCH["small"] = ("sbuf", [128, _a], "float32")
SCRATCH["psA"] = SCRATCH["psB"] = ("psum", [128, 2048], "float32")
for _t in range(R + 1):
    SCRATCH["tq%d" % _t] = ("sbuf", [128, C], F4)
    SCRATCH["tp%d" % _t] = ("sbuf", [128, C], U8)
SENT = [("tq", "aq", F4, C), ("tp", "ap", U8, C), ("ql", "al", "uint16", 24), ("qo", "ao", "uint16", 20)]
for _t in range(R):
    for _s, _d, _k, _n in SENT:
        if _s[0] == "q": SCRATCH["%s%d" % (_s, _t)] = ("sbuf", [128, _n], _k)
        SCRATCH["%s%d" % (_d, _t)] = ("sbuf", [128, _n], _k)
NDMA = 12
SEMAPHORES = ["cv", "cs", "ct", "cg"] + ["d%d" % k for k in range(NDMA)] + ["%s_%s%d" % (a, b[0][1], t) for a in ("r", "l") for b in SENT for t in range(R)]


def rank_program(g, core, T, topo):
    rank = T.rank_of(core)
    if rank is None:
        return
    OP, AF = AluOpType, ActivationFunctionType
    eng = {"v": g.vector, "s": g.scalar, "t": g.tensor, "g": g, "y": g.sync}
    csem = {"v": "cv", "s": "cs", "t": "ct", "g": "cg"}
    count = {}
    known = {q: {} for q in eng}
    known["far"] = {}
    log = {}
    serial = [0]

    def apart(r, o):
        if r[2] <= o[1] or o[2] <= r[1]: return True
        return r[3] > 1 and r[3] == o[3] and (r[1] - o[1]) % r[3] != 0

    def psum(r): return r[0] in ("psA", "psB")

    def widen(r):
        return (r[0], r[1] // 512 * 512, (r[2] + 511) // 512 * 512, 1) if psum(r) else r

    def settle(q, reads, writes):
        need = {}
        for w, rs in ((False, reads), (True, writes)):
            for r in rs:
                for o in log.get(r[0], ()):
                    if apart(widen(r), o["r"]): continue
                    if not (w or o["w"]) and not (psum(r) and o["q"] != q): continue
                    need[o["n"]] = o
        for n in sorted(need, reverse=True):
            o = need[n]
            if known[q].get(o["sem"], 0) >= o["val"]: continue
            eng[q].wait_ge(T.sem[o["sem"]], o["val"])
            for k, v in list(o["clock"].items()) + [(o["sem"], o["val"])]:
                known[q][k] = max(known[q].get(k, 0), v)

    def note(q, reads, writes, sem, val):
        serial[0] += 1
        clock = dict(known[q])
        for w, rs in ((False, reads), (True, writes)):
            for r in rs:
                r = widen(r)
                old = log.get(r[0], [])
                if w and r[3] == 1: old = [o for o in old if not (r[1] <= o["r"][1] and o["r"][2] <= r[2])]
                log[r[0]] = old + [{"r": r, "w": w, "q": q, "sem": sem, "val": val, "clock": clock, "n": serial[0]}]

    def run(q, call, reads, writes):
        settle(q, reads, writes)
        s = csem[q]
        count[s] = count.get(s, 0) + 1
        call().then_inc(T.sem[s], 1)
        note(q, reads, writes, s, count[s])

    def B(name, a=0, b=None, step=1):
        x, y = PART.get(name, (0, 0))
        return ("small", x + a, y if b is None else x + b, step) if y else (name, a, SCRATCH[name][1][1] if b is None else b, step)

    def L(name, buf="lists"): return B(buf, LAT[name][0], LAT[name][1])

    def ap(r):
        return T[r[0]][:, r[1]:r[2]] if r[3] == 1 else T[r[0]][:, r[1]:r[2]:r[3]]

    def ind(r, off): return ap(r).indirect(ap(off))
    def sc(x): return ap(x) if isinstance(x, tuple) else x
    def rd(*xs): return [x for x in xs if isinstance(x, tuple)]

    def fill(out, c): run("v", lambda: g.vector.memset(ap(out), c), [], [out])
    def copy(out, i): run("v", lambda: g.vector.tensor_copy(ap(out), ap(i)), [i], [out])
    def copyi(out, i, off): run("v", lambda: g.vector.tensor_copy(ap(out), ind(i, off)), [i, off], [out])
    def tt(out, a, b, op): run("v", lambda: g.vector.tensor_tensor(ap(out), ap(a), ap(b), op), [a, b], [out])
    def tti(out, a, off, b, op): run("v", lambda: g.vector.tensor_tensor(ap(out), ind(a, off), ap(b), op), [a, off, b], [out])
    def ts(out, a, s1, op, s2=None, op1=None):
        if op1 is None: run("v", lambda: g.vector.tensor_scalar(ap(out), ap(a), sc(s1), None, op), [a] + rd(s1), [out])
        else: run("v", lambda: g.vector.tensor_scalar(ap(out), ap(a), sc(s1), sc(s2), op, op1), [a] + rd(s1, s2), [out])
    def scan(out, keep, a): run("v", lambda: g.vector.tensor_tensor_scan(ap(out), ap(keep), ap(a), 0.0, OP.mult, OP.add), [keep, a], [out])
    def quant(q, p, i): run("v", lambda: g.vector.quantize_mx(ap(q), ap(p), ap(i)), [i], [q, p])
    def mm(out, a, asc, b, bsc): run("t", lambda: g.tensor.matmul_mx(ap(out), ap(a), ap(asc), ap(b), ap(bsc), True, True), [a, asc, b, bsc], [out])
    def act(out, i): run("s", lambda: g.scalar.activation(ap(out), ap(i), AF.Copy), [i], [out])
    def actm(out, i, k): run("s", lambda: g.scalar.activation(ap(out), ap(i), AF.Copy, scale=k), [i], [out])
    def acta(out, i, k): run("s", lambda: g.scalar.activation(ap(out), ap(i), AF.Identity, bias=k), [i], [out])
    def acti(out, i, off): run("s", lambda: g.scalar.activation(ap(out), ind(i, off), AF.Copy), [i, off], [out])
    def pick(q, p, i, ip, off):
        run("v", lambda: g.vector.tensor_copy(ap(q).bitcast(dt.uint32), ap(i).bitcast(dt.uint32).indirect(ap(off))), [i, off], [q])
        acti(p, ip, off)
    def iota(out, pattern, base, cm): run("g", lambda: g.iota(ap(out), pattern, base, cm), [], [out])
    def iotaf(out, pattern, base, cm): run("g", lambda: g.iota(ap(out), pattern, base, cm, allow_small_or_imprecise_dtypes=True), [], [out])
    def keep(out, i, pattern, op, base, cm): run("g", lambda: g.affine_select(ap(out), ap(i), pattern, op, 0.0, base, cm), [i], [out])
    def units(name, ones):
        for b in range(4): keep(B(name, 512 * b, 512 * b + 512), B(ones), [[1, 512]], OP.is_equal, -b, -4)
    ndma = [0]

    def dma(pairs, reads, writes):
        s = "d%d" % ndma[0]
        ndma[0] += 1
        for q in sorted({p[0] for p in pairs}): settle(q, reads, writes)
        for q, o, i in pairs: eng[q].dma_start(o, i).then_inc(T.sem[s], 16)
        count[s] = 16 * len(pairs)
        note(pairs[0][0], reads, writes, s, count[s])

    def send(k, t):
        s, d, kind, n = SENT[k]
        dst, src = T.cores[(rank + STEP[t]) % N], "%s%d" % (s, t)
        settle("g", [B(src)], [])
        i, o = T[src][:, :], T["%s%d" % (d, t)][:, :]
        if kind == F4: i, o = i.bitcast(dt.uint8), o.bitcast(dt.uint8)
        ls, to = "l_%s%d" % (s[1], t), topo.addr(dst)
        g.remote_dma(o, i, T.sem["r_%s%d" % (s[1], t)], T.sem[ls], to[1], to[0], topo.mask(core, dst))
        count[ls] = len(topo.engines(core, dst))

    def expect(k, t):
        s, d, kind, n = SENT[k]
        rs = "r_%s%d" % (s[1], t)
        count[rs] = len(topo.engines(T.cores[(rank - STEP[t]) % N], core))
        note("far", [], [B("%s%d" % (d, t))], rs, count[rs])

    def plane(name, b): return B(name, PW * b, PW * b + PW)
    def body(name, b): return B(name, PW * b, PW * b + C)
    def side(name, b): return B(name, 128 * b, 128 * b + 128)

    dma([("y", T.xt0[:, :], T.x[:, :])], [], [B("xt0")])
    dma([("s", T.ut[:, :], T.u[:, :])], [], [B("ut")])
    dma([("ys"[k % 2], T.cdf[k:128:16, :], T.cd[:, :]) for k in range(16)], [], [B("cdf")])
    settle("y", [B("xt0")], [])
    settle("s", [B("ut"), B("cdf")], [])
    dma([("y", T.wq[:, :].bitcast(dt.uint8), T.wc[:, :])], [], [B("wq")])
    dma([("s", T.wp[:, :], T.ws[:, :])], [], [B("wp")])
    dma([("s", T.vt[:, :], T.v[:, :])], [], [B("vt")])

    iota(B("pi"), [[0, 1]], 0, 1)
    a = 0
    while a < len(LISTS):
        e = a
        while e < len(LISTS) and LISTS[e][4] == LISTS[a][4]: e += 1
        fill(B("lj", LAT[LISTS[a][0]][0], LAT[LISTS[e - 1][0]][1]), LISTS[a][4])
        a = e
    for s, n, p, b, k in LISTS: iota(L(s, "li"), p, b, 0)
    fill(B("co", 0, 48), -767)
    fill(B("co", 48, 72), -383)
    iota(B("ia"), [[0, 48], [1, 16]], 128, -1)
    fill(B("one"), 1.0)
    for k in range(3): keep(B("rs", 384 * k, 384 * k + 384), B("one", 0, 384), [[0, 24], [1, 16]], OP.not_equal, 0, 0)
    for k, n in ((0, 15), (1, 31), (2, 16)): ts(B("pm", k, k + 1), B("pi"), n, OP.bitwise_and)
    copy(B("fc"), B("pm"))
    pm, pr, po = B("fc", 0, 1), B("fc", 1, 2), B("fc", 2, 3)
    ts(B("lk"), B("lj"), pm, OP.mult)
    tt(B("lk"), B("lk"), B("li"), OP.add)
    copy(B("lists"), B("lk", 0, LU))
    x = LAT["an"][0]
    ts(B("lv"), B("lk", x, x + 72), 12, OP.arith_shift_right)
    quant(B("uq"), B("up"), B("ut"))
    tt(B("lw"), B("lv"), B("co"), OP.mult)
    pick(B("urq"), B("urp"), B("uq"), B("up"), L("lu"))
    tt(B("lx"), B("lw"), B("lk", x + 72, x + 144), OP.add)
    ts(B("ia"), B("ia"), 15, OP.bitwise_and)
    copy(B("lcb"), B("lx"))
    ts(B("dg"), B("ia"), 0.0, OP.is_equal)
    units("et", "one")
    fill(B("sb", C, PW), 0.0)
    fill(B("onen"), -1.0)
    fill(B("zero"), 0.0)

    def lists_of_candidates():
        tti(B("c1", 0, 768), B("cdf"), B("lcb", 0, 48), B("dg"), OP.mult)
        scan(B("c2", 0, 768), B("rs", 0, 768), B("c1", 0, 768))
        ts(B("k1"), B("c2", 15, 768, 16), 171.0, OP.mult)
        ts(B("k3"), B("c2", 15, 768, 16), 16.0, OP.mult)
        ts(B("k2"), B("k1"), 12, OP.arith_shift_right)
        ts(B("fr"), pm, 0.0, OP.is_equal, 385.0, OP.mult)
        ts(B("k2"), B("k2"), -383.0, OP.mult)
        tt(B("ke"), B("k2"), B("k3"), OP.add)
        ts(B("ke", 0, 2), B("ke", 0, 2), B("fr"), OP.add)
        copy(B("lc"), B("ke"))

    def lists_inside():
        ts(B("k2"), B("ke"), 15, OP.bitwise_and)
        tt(B("sel", 96, 144), B("ke"), L("ep", "lk"), OP.is_equal)
        ts(B("kt"), B("ke"), -1.0, OP.mult, 386.0, OP.add)
        ts(B("kf"), B("k2"), pm, OP.is_equal)
        ts(B("k3"), B("ke"), 16.0, OP.add)
        tt(B("kg"), B("kf"), B("sel", 96, 144), OP.subtract)
        tt(B("kt"), B("kt"), B("kf"), OP.mult)
        ts(B("ks"), B("sel", 96, 144), 14.0, OP.mult)
        tt(B("sel", 0, 48), B("kg"), B("k3"), OP.mult)
        tt(B("kt"), B("kt"), B("ke"), OP.add)
        ts(B("sel", 144, 192), B("ke"), -float(C), OP.add)
        tt(B("sel", 48, 96), B("kt"), B("ks"), OP.add)
        tt(B("seld"), B("sel", 1, 192, 2), B("sel", 0, 192, 2), OP.subtract)

    def table():
        iotaf(B("i6"), [[1, 24], [32, 16]], 16, 0)
        fill(B("tbl", C, 400), 0.0)
        fill(B("tbl", 386, 387), UNIT)
        acta(B("tbl", 0, C), B("i6"), UNIT)
        acta(B("tbl", 400, 800), B("tbl", 0, 400), UNIT)
        iota(B("jj"), [[1, 32]], 0, 0)
        iotaf(B("jid"), [[1, C]], -192, 0)
        keep(B("rq"), B("one", 0, 128), [[0, 4], [1, 32]], OP.not_equal, 0, 0)
        keep(B("r5"), B("one", 0, 120), [[0, 24], [1, 5]], OP.not_equal, 0, 0)
        iotaf(B("cls"), [[1, 4], [0, 32]], 0, 0)
        units("en", "onen")

    def late_constants():
        fill(B("own", 0, 16), 0.0)
        fill(B("y1", 0, 16), 0.0)
        fill(B("y1", 400, YW), 0.0)
        fill(B("e1"), 0.0)
        for b in range(4):
            for name in ("fn", "ma", "mb", "mc"): act(B(name, PW * b + C, PW * b + PW), B("zero"))
            act(B("rp", RW * b + A, RW * b + RW), B("zero"))
        return [lambda: fill(B("d2", 0, 16), 0.0), lambda: fill(B("dm"), 9.0), lambda: fill(B("w2"), 1.0),
                lambda: ts(B("ja"), B("jj"), po, OP.subtract, 0.0, OP.is_ge),
                lambda: ts(B("jb"), B("jj"), pr, OP.subtract, 0.0, OP.is_ge),
                lambda: ts(B("jc"), B("jj"), po, OP.subtract, 16.0, OP.is_ge),
                lambda: tt(B("mk", 0, 32), B("ja"), B("jb"), OP.subtract),
                lambda: tt(B("mk", 32, 64), B("jb"), B("jc"), OP.subtract),
                lambda: copy(B("mk", 64, 128), B("mk", 0, 64)),
                lambda: copy(B("mk", 128, 256), B("mk", 0, 128)),
                lambda: quant(B("nq"), B("npl"), B("en"))]

    def leave(k):
        for q in (k // 16, k // 16 + 1): ts(B("e1", q, 480, 32), B("y1", 17 + 16 * q, 32 + 16 * q), B("dg", q % 16, q % 16 + 1), OP.mult)

    def settled(m):
        ts(B("e2", m, C, 16), B("d2", 16 + 32 * m, 40 + 32 * m), B("dg", m, m + 1), OP.mult)

    for t in range(R):
        tq, tp, aq, apl, al, ao = ["%s%d" % (s, t) for s in ("tq", "tp", "aq", "ap", "al", "ao")]
        if t == 0:
            quant(B("xq"), B("xp"), B("xt0"))
            pick(B(tq), B(tp), B("xq"), B("xp"), L("lnat"))
        else:
            for h in (0, 192): quant(B(tq, h, h + 192), B(tp, h, h + 192), B("xt", 4 * h, 4 * h + 768))
        for h, k in ((0, 0), (192, 512)):
            mm(B("psA", k, k + 192), B("urq"), B("urp"), B(tq, h, h + 192), B(tp, h, h + 192))
            act(B("sb", h, h + 192), B("psA", k, k + 192))
        send(0, t)
        send(1, t)
        if t == 0:
            lists_of_candidates()
            table()
        tt(B("c1", 768, 960), B("psA", 0, 192), B("dg", 0, 192), OP.mult)
        tti(B("c1", 0, 768), B("sb"), B("lc"), B("dg"), OP.mult)
        tt(B("c1", 960, 1152), B("psA", 512, 704), B("dg", 0, 192), OP.mult)
        scan(B("c2"), B("rs"), B("c1"))
        if t == 0: lists_inside()
        for h in (0, 1): tt(B("da", 24 * h, 24 * h + 24), B("c2", 16 * h + 15, 768, 32), B("c2", 783, 1152, 16), OP.subtract)
        for h in (0, 1): tt(B("db", 24 * h, 24 * h + 24), B("c2", 783, 1152, 16), B("c2", 16 * h + 15, 768, 32), OP.subtract)
        tt(B("dc"), B("da"), B("db"), OP.max)
        tt(B("se"), B("dc", 24, 48), B("dc", 0, 24), OP.is_lt)
        for h in (0, 24, 48): tt(B("sm", h, h + 24), B("seld", h, h + 24), B("se"), OP.mult)
        tt(B("sx", 0, 72), B("sm", 0, 72), B("sel", 0, 144, 2), OP.add)
        tt(B("sm", 72, 96), B("seld", 72, 96), B("se"), OP.mult)
        for h in (0, 12): tt(B("gg", h, h + 12), B("sx", 49, 72, 2), B("sx", 2 * h, 2 * h + 24, 2), OP.mult)
        tt(B("sx", 72, 96), B("sm", 72, 96), B("sel", 144, 192, 2), OP.add)
        tt(B("sx", 1, 48, 2), B("sx", 1, 48, 2), B("gg"), OP.add)
        copy(B("lie"), B("sx", 0, 48))
        spare = late_constants() if t == 0 else []
        if t == 0: quant(B("eq"), B("ep"), B("et"))
        for x, y in ((0, 4), (4, 10), (10, 24)): acti(B("own", 16 + 16 * x, 16 + 16 * y), B("tbl"), B("lie", 24 + x, 24 + y))
        for b in range(4):
            mm(B("psB", 512 * b, 512 * b + C), side("eq", b), side("ep", b), B(tq), B(tp))
            act(body("fp", b), B("psB", 512 * b, 512 * b + C))
        for k in range(32, C, 32):
            tti(B("y1", 16 + k, 48 + k), B("own" if k == 32 else "y1", 0, 16 + k), B("lie", k // 16, k // 16 + 2), B("own", 16 + k, 48 + k), OP.add)
            if k == 32: copy(B("y1", 16, 48), B("own", 16, 48))
            else: leave(k - 64)
            for f in spare[:2]: f()
            spare = spare[2:]
        leave(C - 64)
        leave(C - 32)
        scan(B("c2", 0, 480), B("rs", 0, 480), B("e1"))
        copy(B("d2", 16, 48), B("y1", 16, YW, 16))
        copy(B("lb"), B("c2", 15, 480, 16))
        for m in range(1, M):
            tti(B("d2", 16 + 32 * m, 48 + 32 * m), B("d2", 0, 16 + 32 * m), B("lb", 2 * m - 2, 2 * m), B("y1", 16 + m, YW, 16), OP.add)
            settled(m - 1)
            for f in spare[:1]: f()
            spare = spare[1:]
        settled(M - 1)
        scan(B("c2", 0, C), B("rs", 0, C), B("e2"))
        ts(B("dw"), B("c2", 15, C, 16), 1 / UNIT, OP.mult)
        ts(B("dm", 0, 24), B("dw"), 3, OP.bitwise_and)
        ts(B("pos"), B("dm", 0, 24), 0.0, OP.is_gt)
        tti(B("ind"), B("dm"), L("lcls"), B("cls"), OP.is_equal)
        tt(B("ls"), B("sx", 72, 96), B("pos"), OP.mult)
        scan(B("inc"), B("rq"), B("ind"))
        ts(B("ql%d" % t), B("ls"), float(C), OP.add)
        send(2, t)
        copyi(B("tb"), B("inc"), L("ltot"))
        tt(B("pr"), B("ind"), B("inc"), OP.mult)
        run("v", lambda: g.vector.transpose(ap(B("tv")), ap(B("tb"))), [B("tb")], [B("tv")])
        tt(B("ps_"), B("pr", 0, 64), B("pr", 64, 128), OP.add)
        tti(B("w1"), B("tv"), L("ldup"), B("mk"), OP.mult)
        tt(B("pu", 4, 120, 5), B("ps_", 0, 24), B("ps_", 32, 56), OP.add)
        scan(B("bs"), B("w2"), B("w1"))
        for c in range(4): ts(B("pu", c, 120, 5), B("ind", 32 * c, 32 * c + 24), B("bs", 64 * c + 31, 64 * c + 32), OP.mult)
        scan(B("pv"), B("r5"), B("pu"))
        ts(B("lpl"), B("pv", 4, 120, 5), -1.0, OP.add)
        ts(B("lpx"), B("pv", 4, 120, 5), -1.0, OP.add, float(A), OP.min)
        for k in range(4): expect(k, t)
        for b in range(4):
            mm(B("psA", 512 * b, 512 * b + C), side("nq", b), side("npl", b), B(aq), B(apl))
            for name in ("fn", "fo")[:1 + (b < 2)]: act(body(name, b), B("psA", 512 * b, 512 * b + C))
        for b in (2, 3): acti(body("mg", b), plane("fn", b), B(al))
        for b in (0, 1): tti(B("pt", b, 4 * C, 4), plane("fn", b), B(al), body("fo", b), OP.subtract)
        for b in (2, 3): tt(B("pt", b, 4 * C, 4), body("mg", b), B("psA", 512 * b, 512 * b + C), OP.subtract)
        for h, ps in ((0, "psB"), (192, "psA")):
            quant(B("pq", h, h + 192), B("pz", h, h + 192), B("pt", 4 * h, 4 * h + 768))
            mm(B(ps, 0, 192), side("eq", 0), side("ep", 0), B("pq", h, h + 192), B("pz", h, h + 192))
            act(B("ma", h, h + 192), B(ps, 0, 192))
        for b in range(1, 4):
            mm(B("psB", 512 * b, 512 * b + C), side("eq", b), side("ep", b), B("pq"), B("pz"))
            act(body("ma", b), B("psB", 512 * b, 512 * b + C))
            if b > 1: acti(body("mg", b), plane("ma", b), B(al))
        run("v", lambda: g.vector.tensor_copy(ind(B("of"), B("lpl")), ap(B("jid"))), [B("jid"), B("lpl")], [B("of")])
        order = [lambda: tt(B("og"), B("of", 0, A), B("dg", 0, A), OP.mult), lambda: scan(B("oh"), B("rs", 0, A), B("og")),
                 lambda: ts(B("qo%d" % t), B("oh", 15, A, 16), 192.0, OP.add)]
        for src, dst in (("ma", "mb"), ("mb", "mc"), ("mc", "mb")):
            if src != "ma":
                for b in (2, 3): acti(body("mg", b), plane(src, b), B(al))
            for b in (0, 1):
                if src == "ma":
                    order[b]()
                    copy(body("md", b), body("ma", b))
                tti(body(dst, b), plane(src, b), B(al), body("md", b), OP.add)
            if src == "ma":
                order[2]()
                send(3, t)
            for b in (2, 3): tt(body(dst, b), body("mg", b), B("psB", 512 * b, 512 * b + C), OP.add)
        for b in range(3): acti(B("mt", b, 4 * A, 4), plane("mb", b), B(ao))
        acti(B("mt", 3, 640, 4), plane("mb", 3), B(ao, 0, 10))
        copyi(B("mt", 643, 1280, 4), plane("mb", 3), B(ao, 10, 20))
        for h, ps in ((0, "psA"), (160, "psB")):
            quant(B("mq", h, h + 160), B("mp", h, h + 160), B("mt", 4 * h, 4 * h + 640))
            mm(B(ps, 0, 160), side("wq", 0), side("wp", 0), B("mq", h, h + 160), B("mp", h, h + 160))
            actm(B("rp", h, h + 160), B(ps, 0, 160), 0.015625)
        if t == R - 1: quant(B("vq"), B("vp"), B("vt"))
        for b in range(1, 4):
            mm(B("psA", 512 * b, 512 * b + A), side("wq", b), side("wp", b), B("mq"), B("mp"))
            actm(B("rp", RW * b, RW * b + A), B("psA", 512 * b, 512 * b + A), 0.015625)
        for b in range(4):
            tti(B("xt", b, 4 * C, 4), B("rp", RW * b, RW * b + RW), B("lpx"), body("fp", b), OP.add)

    quant(B("tq%d" % R), B("tp%d" % R), B("xt"))
    pick(B("oq"), B("op"), B("tq%d" % R), B("tp%d" % R), B("lcb", 48, 72))
    dma([("y", T.oc[:, :], T.oq[:, :].bitcast(dt.uint8))], [B("oq")], [])
    dma([("s", T.osc[4 * k:4 * k + 4, :], T.op[32 * k:32 * k + 4, :]) for k in range(4)], [B("op")], [])
    mm(B("psB", 0, C), B("vq"), B("vp"), B("oq"), B("op"))
    copy(B("yo"), B("psB", 0, C))
    dma([("y", T.y[:, :], T.yo[:, :])], [B("yo")], [])
    for s in sorted(count): g.wait_ge(T.sem[s], count[s])
